import numpy as np
import ml_dtypes


def mxq(x, axis, fmt="e4m3"):
    dtype, down = {"e4m3": (ml_dtypes.float8_e4m3fn, 7), "e5m2": (ml_dtypes.float8_e5m2, 14)}[fmt]
    v = np.moveaxis(np.asarray(x, np.float32).astype(ml_dtypes.bfloat16).astype(np.float64), axis, -1)
    blocks = v.reshape(v.shape[:-1] + (-1, 32))
    amax = np.abs(blocks).max(-1, keepdims=True)
    byte = np.maximum(np.where(amax > 0, np.frexp(amax)[1] - 1 + 127, 0) - down, 1)
    scale = np.exp2(byte - 127.0)
    codes = (blocks / scale).astype(np.float32).astype(dtype).astype(np.float64)
    return np.moveaxis((codes * scale).reshape(v.shape), -1, axis)


WIDE = False


def mx_kscale(k):
    if not WIDE:
        return np.ones(k)
    levels = np.array([10, -10, 5, -5, 0])
    if k % 512:
        return np.exp2(np.random.permutation(np.resize(levels, k // 32))).repeat(32)
    a = np.empty((k // 512, 16))
    for p in range(k // 512):
        a[p, :8] = np.random.permutation(np.resize(levels, 8))
        for g in range(8):
            far = levels[np.abs(levels - a[p, g]) >= 10]
            a[p, g + 8] = far[np.random.randint(len(far))]
    return np.exp2(a.ravel()).repeat(32)


def f64(x):
    return np.asarray(x).astype(np.float64)


def striped(idx):
    return np.tile(idx.reshape(-1, 16).T, (8, 1)).astype(np.uint16)


def unstriped(offs):
    return offs[:16].T.reshape(-1).astype(np.int64)


def pack_weight(w):
    k, n = w.shape
    w = f64(np.asarray(w, np.float32).astype(ml_dtypes.bfloat16)).reshape(k // 32, 32, n)
    amax = np.abs(w).max(1)
    byte = np.clip(np.where(amax > 0, np.frexp(amax)[1] - 1 + 127 - 7, 1), 1, 254)
    scaled = (w * np.exp2(127.0 - byte)[:, None, :]).reshape(k, n).astype(np.float32)
    words = np.ascontiguousarray(scaled.reshape(k // 512, 128, 4, n).transpose(0, 1, 3, 2)).astype(ml_dtypes.float8_e4m3fn).view(np.uint8)
    return words, np.ascontiguousarray(byte.astype(np.uint8).reshape(k // 512, 16, n))


def unpack_weight(words, scales):
    g, p, n, _ = words.shape
    vals = np.ascontiguousarray(words).view(ml_dtypes.float8_e4m3fn).astype(np.float64) * np.repeat(np.exp2(scales.astype(np.float64) - 127.0), 8, axis=1)[..., None]
    return vals.transpose(0, 1, 3, 2).reshape(g * 512, n)


K, T, S, D, H, N = 1024, 1024, 512, 3, 512, 128


def setup_inputs():
    n = np.random.standard_normal
    s = mx_kscale(K)[:, None]
    u = mx_kscale(H)
    packed_w2 = pack_weight(n((H, N)) / np.sqrt(H) / u[:, None])
    return {
        "xT": (n((K, T)) * s).astype(np.float32),
        "w1": (n((K, H)) / np.sqrt(K) / s * u).astype(np.float32),
        "w2_words": packed_w2[0],
        "w2_scales": packed_w2[1],
        "taps": (n((H, D)) / np.sqrt(D)).astype(np.float32),
        "offs": striped(np.random.permutation(T)[:S]),
    }


def reference(xT, w1, w2_words, w2_scales, taps, offs):
    xq = mxq(f64(xT)[:, unstriped(offs)], 0, "e4m3")
    h = mxq(f64(w1), 0, "e4m3").T @ xq
    z = f64(taps)[:, 0:1] * h + f64(taps)[:, 1:2] * (np.pad(h, ((0, 0), (1, 0)))[:, :S]) + f64(taps)[:, 2:3] * (np.pad(h, ((0, 0), (2, 0)))[:, :S])
    return unpack_weight(w2_words, w2_scales).T @ mxq(z, 0, "e4m3")

@@ -1,0 +1,209 @@
+from contextlib import ExitStack
+
+import concourse.mybir as mybir
+
+K, T, S, D, H, N = 1024, 1024, 512, 3, 512, 128
+FLOPS = 2 * K * H * S + 2 * H * N * S
+
+F32 = mybir.dt.float32
+BF16 = mybir.dt.bfloat16
+I32 = mybir.dt.int32
+U32 = mybir.dt.uint32
+U16 = mybir.dt.uint16
+U8 = mybir.dt.uint8
+FP8X4 = mybir.dt.float8_e4m3fn_x4
+COPY = mybir.ActivationFunctionType.Copy
+MULT = mybir.AluOpType.mult
+ADD = mybir.AluOpType.add
+
+P = 128
+PACK = 4
+K_PASS = P * PACK
+PASSES = K // K_PASS
+
+X_PIECES = [(0, 0, 512, 256), (0, 512, 256, 128), (0, 768, 256, 128), (1, 0, 512, 256), (1, 512, 256, 128), (1, 768, 256, 128)]
+W_PIECES = [(0, 0, 64), (0, 64, 64), (1, 0, 64), (1, 64, 32), (1, 96, 32)]
+HALF = S // 2
+QUARTER = S // 4
+
+
+def tile_picked_dconv_none_e_kernel(tc, xT, w1, w2_words, w2_scales, taps, offs, out):
+    nc = tc.nc
+
+    def cast(engine_is_scalar, dst, src):
+        if engine_is_scalar:
+            nc.scalar.activation(out=dst, in_=src, func=COPY)
+        else:
+            nc.vector.tensor_copy(out=dst, in_=src)
+
+    with ExitStack() as ctx:
+        keep = ctx.enter_context(tc.tile_pool(name="keep", bufs=1))
+        psum = ctx.enter_context(tc.psum_pool(name="psum", bufs=1))
+
+        offsets = keep.tile([P, S // 16], U16, name="offsets")
+        taps_sb = keep.tile([P, PACK * D], F32, name="taps_sb")
+        x_raw = []
+        for n, (g, t0, nt, ns) in enumerate(X_PIECES):
+            raw = keep.tile([P, PACK, nt], F32, name=f"x_raw{n}")
+            rows = xT[g * K_PASS : (g + 1) * K_PASS, t0 : t0 + nt]
+            nc.sync.dma_start(out=raw[:], in_=rows.rearrange("(p j) c -> p j c", j=PACK))
+            x_raw.append(raw)
+            if n == 0:
+                nc.sync.dma_start(offsets[:], offs)
+            if n == 2:
+                nc.sync.dma_start(out=taps_sb[:], in_=taps.rearrange("(p t) d -> p (t d)", t=PACK))
+        w_raw = []
+        for n, (g, m0, nm) in enumerate(W_PIECES):
+            raw = keep.tile([P, PACK, PACK * nm], F32, name=f"w_raw{n}")
+            rows = w1[g * K_PASS : (g + 1) * K_PASS, PACK * m0 : PACK * (m0 + nm)]
+            nc.sync.dma_start(out=raw[:], in_=rows.rearrange("(p j) c -> p j c", j=PACK))
+            w_raw.append(raw)
+
+        x_scales = keep.tile([P, T], U8, name="x_scales", align_bytes=64)
+        nc.gpsimd.memset(x_scales[:], 0)
+        w2_plane = keep.tile([P, N], U8, name="w2_plane", align_bytes=64)
+        nc.gpsimd.memset(w2_plane[:], 0)
+        w2_codes = keep.tile([P, N], U32, name="w2_codes", align_bytes=64)
+        nc.sync.dma_start(out=w2_codes[:].bitcast(I32), in_=w2_words[0].rearrange("p n t -> p (n t)").bitcast(I32))
+        for q in range(4):
+            nc.sync.dma_start(
+                out=w2_plane[32 * q : 32 * q + 4, :].bitcast(I32),
+                in_=w2_scales[0, 4 * q : 4 * q + 4, :].bitcast(I32),
+            )
+
+        def tap(t, d):
+            return taps_sb[:, D * t + d : D * t + d + 1]
+
+        x_codes = [keep.tile([P, T], U32, name=f"x_codes{g}", align_bytes=64) for g in range(PASSES)]
+        picked_codes = [keep.tile([P, S], U32, name=f"picked_codes{g}", align_bytes=64) for g in range(PASSES)]
+        picked_scales = keep.tile([P, S], U8, name="picked_scales", align_bytes=64)
+        for n, (g, t0, nt, ns) in enumerate(X_PIECES):
+            shares = ((False, ns, nt), (True, 0, ns))
+            grouped = [keep.tile([P, PACK * (b - a)], BF16, name=f"x_grouped{n}_{a}", align_bytes=64) for on_scalar, a, b in shares]
+            for (on_scalar, a, b), dst in zip(shares, grouped):
+                cast(
+                    on_scalar,
+                    dst[:].rearrange("p (c i j) -> p c j i", i=4, j=PACK),
+                    x_raw[n][:, :, a:b].rearrange("p j (c i) -> p c j i", i=4),
+                )
+            for (on_scalar, a, b), src in zip(shares, grouped):
+                nc.vector.quantize_mx(
+                    out=x_codes[g][:, t0 + a : t0 + b].bitcast(FP8X4),
+                    scales=x_scales[PACK * g : P, t0 + a : t0 + b],
+                    in_=src[:],
+                )
+            if t0 + nt == T:
+                if g == PASSES - 1:
+                    nc.vector.tensor_copy(out=picked_scales[:], in_=x_scales[:].indirect(offsets[:]))
+                nc.vector.tensor_copy(out=picked_codes[g][:], in_=x_codes[g][:].indirect(offsets[:]))
+
+        h = [psum.tile([P, S], F32, name=f"h{t}") for t in range(PACK)]
+        w_codes = [keep.tile([P, H], U32, name=f"w_codes{g}", align_bytes=64) for g in range(PASSES)]
+        w_scales = [keep.tile([P, H], U8, name=f"w_scales{g}", align_bytes=64) for g in range(PASSES)]
+
+        def cast_w(on_scalar, grouped, base, n):
+            g, m0, nm = W_PIECES[n]
+            cast(
+                on_scalar,
+                grouped[:, :, PACK * (m0 - base) : PACK * (m0 - base + nm)].rearrange("p t (m j) -> p m j t", j=PACK),
+                w_raw[n][:].rearrange("p j (m t) -> p m j t", t=PACK),
+            )
+
+        def quantize_w(g, grouped, base, nm, t):
+            cols = slice(P * t + base, P * t + base + nm)
+            nc.vector.quantize_mx(out=w_codes[g][:, cols].bitcast(FP8X4), scales=w_scales[g][:, cols], in_=grouped[:, t, :])
+
+        def first_product(g, t):
+            cols = slice(P * t, P * (t + 1))
+            nc.tensor.matmul_mx(
+                out=h[t][:],
+                lhsT=w_codes[g][:, cols].bitcast(FP8X4),
+                lhsT_scale=w_scales[g][:, cols],
+                rhs=picked_codes[g][:].bitcast(FP8X4),
+                rhs_scale=picked_scales[PACK * g : P, :],
+                start=(g == 0),
+                stop=(g == PASSES - 1),
+            )
+
+        first = keep.tile([P, PACK, P * PACK], BF16, name="w_first", tag="w_shared", align_bytes=64)
+        cast_w(True, first, 0, 0)
+        cast_w(True, first, 0, 1)
+        for t in range(PACK):
+            quantize_w(0, first, 0, P, t)
+            if t < PACK - 1:
+                first_product(0, t)
+        low = keep.tile([P, PACK, 64 * PACK], BF16, name="w_low", align_bytes=64)
+        high = keep.tile([P, PACK, 64 * PACK], BF16, name="w_high", tag="w_shared", align_bytes=64)
+        cast_w(True, low, 0, 2)
+        cast_w(False, high, 64, 3)
+        cast_w(False, high, 64, 4)
+        for t in range(PACK):
+            quantize_w(1, low, 0, 64, t)
+        for t in range(PACK):
+            quantize_w(1, high, 64, 64, t)
+            first_product(1, t)
+            if t == 1:
+                first_product(0, PACK - 1)
+
+        front = keep.tile([P, PACK, HALF], F32, name="front")
+        back0 = keep.tile([P, PACK, HALF], F32, name="back0")
+        back12 = keep.tile([P, PACK, HALF], F32, name="back12")
+
+        def front_tap(t, d):
+            nc.vector.scalar_tensor_tensor(
+                out=front[:, t, d:HALF], in0=h[t][:, 0 : HALF - d], scalar=tap(t, d), in1=front[:, t, d:HALF], op0=MULT, op1=ADD
+            )
+
+        for t in range(PACK):
+            nc.scalar.activation(out=front[:, t, :], in_=h[t][:, 0:HALF], func=COPY, scale=tap(t, 0))
+        for pair in ((0, 1), (2, 3)):
+            for d in (1, 2):
+                for t in pair:
+                    front_tap(t, d)
+        for t in range(PACK):
+            nc.scalar.activation(out=back12[:, t, :], in_=h[t][:, HALF - 1 : S - 1], func=COPY, scale=tap(t, 1))
+            nc.scalar.activation(out=back0[:, t, :], in_=h[t][:, HALF:S], func=COPY, scale=tap(t, 0))
+        for t in range(PACK):
+            nc.vector.scalar_tensor_tensor(
+                out=back12[:, t, :], in0=h[t][:, HALF - 2 : S - 2], scalar=tap(t, 2), in1=back12[:, t, :], op0=MULT, op1=ADD
+            )
+
+        chunks = [(0, HALF), (HALF, QUARTER), (HALF + QUARTER, QUARTER)]
+        z = [keep.tile([P, PACK * w], BF16, name=f"z{n}", align_bytes=64) for n, (c0, w) in enumerate(chunks)]
+
+        def z_view(n):
+            return z[n][:].rearrange("p (c i t) -> p c t i", i=4, t=PACK)
+
+        def by_four(ap):
+            return ap.rearrange("p t (c i) -> p c t i", i=4)
+
+        def back_sum(n):
+            c0, w = chunks[n]
+            cols = slice(c0 - HALF, c0 - HALF + w)
+            nc.vector.tensor_tensor(out=z_view(n), in0=by_four(back12[:, :, cols]), in1=by_four(back0[:, :, cols]), op=ADD)
+
+        def second_product(n):
+            c0, w = chunks[n]
+            z_codes = keep.tile([P, w], U32, name=f"z_codes{n}", align_bytes=64)
+            z_scales = keep.tile([P, w], U8, name=f"z_scales{n}", align_bytes=64)
+            nc.vector.quantize_mx(out=z_codes[:].bitcast(FP8X4), scales=z_scales[:], in_=z[n][:])
+            acc = psum.tile([P, w], F32, name=f"acc{n}")
+            nc.tensor.matmul_mx(
+                out=acc[:],
+                lhsT=w2_codes[:].bitcast(FP8X4),
+                lhsT_scale=w2_plane[:],
+                rhs=z_codes[:].bitcast(FP8X4),
+                rhs_scale=z_scales[:],
+                start=True,
+                stop=True,
+            )
+            result = keep.tile([P, w], F32, name=f"result{n}")
+            nc.scalar.activation(out=result[:], in_=acc[:], func=COPY)
+            nc.sync.dma_start(out=out[:, c0 : c0 + w], in_=result[:])
+
+        nc.scalar.activation(out=z_view(0), in_=by_four(front[:]), func=COPY)
+        back_sum(1)
+        second_product(0)
+        back_sum(2)
+        second_product(1)
+        second_product(2)

@@ -50,8 +50,6 @@ def tile_picked_dconv_none_e_kernel(tc, xT, w1, w2_words, w2_scales, taps, offs,
             x_raw.append(raw)
             if n == 0:
                 nc.sync.dma_start(offsets[:], offs)
-            if n == 2:
-                nc.sync.dma_start(out=taps_sb[:], in_=taps.rearrange("(p t) d -> p (t d)", t=PACK))
         w_raw = []
         for n, (g, m0, nm) in enumerate(W_PIECES):
             raw = keep.tile([P, PACK, PACK * nm], F32, name=f"w_raw{n}")
@@ -60,9 +58,10 @@ def tile_picked_dconv_none_e_kernel(tc, xT, w1, w2_words, w2_scales, taps, offs,
             w_raw.append(raw)
 
         x_scales = keep.tile([P, T], U8, name="x_scales", align_bytes=64)
-        nc.gpsimd.memset(x_scales[:], 0)
+        nc.vector.memset(x_scales[:].bitcast(I32), 0)
+        nc.gpsimd.dma_start(out=taps_sb[:], in_=taps.rearrange("(p t) d -> p (t d)", t=PACK))
         w2_plane = keep.tile([P, N], U8, name="w2_plane", align_bytes=64)
-        nc.gpsimd.memset(w2_plane[:], 0)
+        nc.vector.memset(w2_plane[:].bitcast(I32), 0)
         w2_codes = keep.tile([P, N], U32, name="w2_codes", align_bytes=64)
         nc.sync.dma_start(out=w2_codes[:].bitcast(I32), in_=w2_words[0].rearrange("p n t -> p (n t)").bitcast(I32))
         for q in range(4):
@@ -71,12 +70,23 @@ def tile_picked_dconv_none_e_kernel(tc, xT, w1, w2_words, w2_scales, taps, offs,
                 in_=w2_scales[0, 4 * q : 4 * q + 4, :].bitcast(I32),
             )
 
+        sums = keep.tile([P, PACK, S], F32, name="sums")
+        back0 = keep.tile([P, PACK, HALF], F32, name="back0")
+        nc.vector.memset(sums[:, :, HALF : HALF + 2], 0.0)
+
         def tap(t, d):
             return taps_sb[:, D * t + d : D * t + d + 1]
 
         x_codes = [keep.tile([P, T], U32, name=f"x_codes{g}", align_bytes=64) for g in range(PASSES)]
         picked_codes = [keep.tile([P, S], U32, name=f"picked_codes{g}", align_bytes=64) for g in range(PASSES)]
-        picked_scales = keep.tile([P, S], U8, name="picked_scales", align_bytes=64)
+        picked_scales = []
+
+        def pick_scales(half, tag):
+            plane = keep.tile([P, HALF], U8, name=f"picked_scales{half}", tag=tag, align_bytes=64)
+            columns = HALF // 16
+            nc.vector.tensor_copy(out=plane[:], in_=x_scales[:].indirect(offsets[:, columns * half : columns * (half + 1)]))
+            picked_scales.append(plane)
+
         for n, (g, t0, nt, ns) in enumerate(X_PIECES):
             shares = ((False, ns, nt), (True, 0, ns))
             grouped = [keep.tile([P, PACK * (b - a)], BF16, name=f"x_grouped{n}_{a}", align_bytes=64) for on_scalar, a, b in shares]
@@ -94,79 +104,77 @@ def tile_picked_dconv_none_e_kernel(tc, xT, w1, w2_words, w2_scales, taps, offs,
                 )
             if t0 + nt == T:
                 if g == PASSES - 1:
-                    nc.vector.tensor_copy(out=picked_scales[:], in_=x_scales[:].indirect(offsets[:]))
+                    pick_scales(0, "picked_scales0")
                 nc.vector.tensor_copy(out=picked_codes[g][:], in_=x_codes[g][:].indirect(offsets[:]))
 
-        h = [psum.tile([P, S], F32, name=f"h{t}") for t in range(PACK)]
+        h = [[psum.tile([P, HALF], F32, name=f"h{half}_{t}") for t in range(PACK)] for half in range(2)]
         w_codes = [keep.tile([P, H], U32, name=f"w_codes{g}", align_bytes=64) for g in range(PASSES)]
         w_scales = [keep.tile([P, H], U8, name=f"w_scales{g}", align_bytes=64) for g in range(PASSES)]
 
-        def cast_w(on_scalar, grouped, base, n):
+        def cast_w(on_scalar, grouped, base, n, a=0, b=None):
             g, m0, nm = W_PIECES[n]
+            b = nm if b is None else b
             cast(
                 on_scalar,
-                grouped[:, :, PACK * (m0 - base) : PACK * (m0 - base + nm)].rearrange("p t (m j) -> p m j t", j=PACK),
-                w_raw[n][:].rearrange("p j (m t) -> p m j t", t=PACK),
+                grouped[:, :, PACK * (m0 - base + a) : PACK * (m0 - base + b)].rearrange("p t (m j) -> p m j t", j=PACK),
+                w_raw[n][:, :, PACK * a : PACK * b].rearrange("p j (m t) -> p m j t", t=PACK),
             )
 
         def quantize_w(g, grouped, base, nm, t):
             cols = slice(P * t + base, P * t + base + nm)
             nc.vector.quantize_mx(out=w_codes[g][:, cols].bitcast(FP8X4), scales=w_scales[g][:, cols], in_=grouped[:, t, :])
 
-        def first_product(g, t):
+        def first_product(g, half, t):
             cols = slice(P * t, P * (t + 1))
+            entries = slice(HALF * half, HALF * (half + 1))
             nc.tensor.matmul_mx(
-                out=h[t][:],
+                out=h[half][t][:],
                 lhsT=w_codes[g][:, cols].bitcast(FP8X4),
                 lhsT_scale=w_scales[g][:, cols],
-                rhs=picked_codes[g][:].bitcast(FP8X4),
-                rhs_scale=picked_scales[PACK * g : P, :],
+                rhs=picked_codes[g][:, entries].bitcast(FP8X4),
+                rhs_scale=picked_scales[half][PACK * g : P, :],
                 start=(g == 0),
                 stop=(g == PASSES - 1),
             )
 
         first = keep.tile([P, PACK, P * PACK], BF16, name="w_first", tag="w_shared", align_bytes=64)
         cast_w(True, first, 0, 0)
-        cast_w(True, first, 0, 1)
+        cast_w(True, first, 0, 1, 0, 32)
+        cast_w(False, first, 0, 1, 32, 64)
         for t in range(PACK):
             quantize_w(0, first, 0, P, t)
-            if t < PACK - 1:
-                first_product(0, t)
+            first_product(0, 0, t)
         low = keep.tile([P, PACK, 64 * PACK], BF16, name="w_low", align_bytes=64)
         high = keep.tile([P, PACK, 64 * PACK], BF16, name="w_high", tag="w_shared", align_bytes=64)
         cast_w(True, low, 0, 2)
         cast_w(False, high, 64, 3)
-        cast_w(False, high, 64, 4)
+        cast_w(True, high, 64, 4, 0, 12)
+        cast_w(False, high, 64, 4, 12, 32)
         for t in range(PACK):
             quantize_w(1, low, 0, 64, t)
-        for t in range(PACK):
             quantize_w(1, high, 64, 64, t)
-            first_product(1, t)
-            if t == 1:
-                first_product(0, PACK - 1)
+            first_product(1, 0, t)
+        pick_scales(1, "w_shared")
+        for t in range(PACK):
+            for g in range(PASSES):
+                first_product(g, 1, t)
 
-        front = keep.tile([P, PACK, HALF], F32, name="front")
-        back0 = keep.tile([P, PACK, HALF], F32, name="back0")
-        back12 = keep.tile([P, PACK, HALF], F32, name="back12")
-
-        def front_tap(t, d):
-            nc.vector.scalar_tensor_tensor(
-                out=front[:, t, d:HALF], in0=h[t][:, 0 : HALF - d], scalar=tap(t, d), in1=front[:, t, d:HALF], op0=MULT, op1=ADD
-            )
+        def add_tap(half, t, d, count):
+            first_out = HALF * half + d
+            cols = sums[:, t, first_out : first_out + count]
+            nc.vector.scalar_tensor_tensor(out=cols, in0=h[half][t][:, 0:count], scalar=tap(t, d), in1=cols, op0=MULT, op1=ADD)
 
         for t in range(PACK):
-            nc.scalar.activation(out=front[:, t, :], in_=h[t][:, 0:HALF], func=COPY, scale=tap(t, 0))
+            nc.scalar.activation(out=sums[:, t, 0:HALF], in_=h[0][t][:], func=COPY, scale=tap(t, 0))
         for pair in ((0, 1), (2, 3)):
             for d in (1, 2):
                 for t in pair:
-                    front_tap(t, d)
+                    add_tap(0, t, d, HALF)
         for t in range(PACK):
-            nc.scalar.activation(out=back12[:, t, :], in_=h[t][:, HALF - 1 : S - 1], func=COPY, scale=tap(t, 1))
-            nc.scalar.activation(out=back0[:, t, :], in_=h[t][:, HALF:S], func=COPY, scale=tap(t, 0))
+            nc.scalar.activation(out=sums[:, t, HALF + 2 : S], in_=h[1][t][:, 0 : HALF - 2], func=COPY, scale=tap(t, 2))
+            nc.scalar.activation(out=back0[:, t, :], in_=h[1][t][:], func=COPY, scale=tap(t, 0))
         for t in range(PACK):
-            nc.vector.scalar_tensor_tensor(
-                out=back12[:, t, :], in0=h[t][:, HALF - 2 : S - 2], scalar=tap(t, 2), in1=back12[:, t, :], op0=MULT, op1=ADD
-            )
+            add_tap(1, t, 1, HALF - 1)
 
         chunks = [(0, HALF), (HALF, QUARTER), (HALF + QUARTER, QUARTER)]
         z = [keep.tile([P, PACK * w], BF16, name=f"z{n}", align_bytes=64) for n, (c0, w) in enumerate(chunks)]
@@ -180,14 +188,14 @@ def tile_picked_dconv_none_e_kernel(tc, xT, w1, w2_words, w2_scales, taps, offs,
         def back_sum(n):
             c0, w = chunks[n]
             cols = slice(c0 - HALF, c0 - HALF + w)
-            nc.vector.tensor_tensor(out=z_view(n), in0=by_four(back12[:, :, cols]), in1=by_four(back0[:, :, cols]), op=ADD)
+            nc.vector.tensor_tensor(out=z_view(n), in0=by_four(sums[:, :, c0 : c0 + w]), in1=by_four(back0[:, :, cols]), op=ADD)
 
         def second_product(n):
             c0, w = chunks[n]
             z_codes = keep.tile([P, w], U32, name=f"z_codes{n}", align_bytes=64)
             z_scales = keep.tile([P, w], U8, name=f"z_scales{n}", align_bytes=64)
             nc.vector.quantize_mx(out=z_codes[:].bitcast(FP8X4), scales=z_scales[:], in_=z[n][:])
-            acc = psum.tile([P, w], F32, name=f"acc{n}")
+            acc = psum.tile([P, w], F32, name=f"acc{n}", tag=f"h0_{n}")
             nc.tensor.matmul_mx(
                 out=acc[:],
                 lhsT=w2_codes[:].bitcast(FP8X4),
@@ -199,9 +207,10 @@ def tile_picked_dconv_none_e_kernel(tc, xT, w1, w2_words, w2_scales, taps, offs,
             )
             result = keep.tile([P, w], F32, name=f"result{n}")
             nc.scalar.activation(out=result[:], in_=acc[:], func=COPY)
-            nc.sync.dma_start(out=out[:, c0 : c0 + w], in_=result[:])
+            queue = nc.scalar if n == 2 else nc.sync
+            queue.dma_start(out=out[:, c0 : c0 + w], in_=result[:])
 
-        nc.scalar.activation(out=z_view(0), in_=by_four(front[:]), func=COPY)
+        nc.scalar.activation(out=z_view(0), in_=by_four(sums[:, :, 0:HALF]), func=COPY)
         back_sum(1)
         second_product(0)
         back_sum(2)

@@ -21,8 +21,8 @@ PACK = 4
 K_PASS = P * PACK
 PASSES = K // K_PASS
 
-X_PIECES = [(0, 0, 512, 256), (0, 512, 256, 128), (0, 768, 256, 128), (1, 0, 512, 256), (1, 512, 256, 128), (1, 768, 256, 128)]
-W_PIECES = [(0, 0, 64), (0, 64, 64), (1, 0, 64), (1, 64, 32), (1, 96, 32)]
+X_PIECES = [(0, 0, 512, 256), (0, 512, 256, 128), (0, 768, 256, 128), (1, 0, 512, 256), (1, 512, 256, 128), (1, 768, 128, 128), (1, 896, 128, 0)]
+W_PIECES = [(0, 0, 64, 64), (0, 64, 64, 64), (1, 0, 64, 64), (1, 64, 32, 8), (1, 96, 32, 12)]
 HALF = S // 2
 QUARTER = S // 4
 
@@ -51,7 +51,7 @@ def tile_picked_dconv_none_e_kernel(tc, xT, w1, w2_words, w2_scales, taps, offs,
             if n == 0:
                 nc.sync.dma_start(offsets[:], offs)
         w_raw = []
-        for n, (g, m0, nm) in enumerate(W_PIECES):
+        for n, (g, m0, nm, ns) in enumerate(W_PIECES):
             raw = keep.tile([P, PACK, PACK * nm], F32, name=f"w_raw{n}")
             rows = w1[g * K_PASS : (g + 1) * K_PASS, PACK * m0 : PACK * (m0 + nm)]
             nc.sync.dma_start(out=raw[:], in_=rows.rearrange("(p j) c -> p j c", j=PACK))
@@ -59,7 +59,7 @@ def tile_picked_dconv_none_e_kernel(tc, xT, w1, w2_words, w2_scales, taps, offs,
 
         x_scales = keep.tile([P, T], U8, name="x_scales", align_bytes=64)
         nc.vector.memset(x_scales[:].bitcast(I32), 0)
-        nc.gpsimd.dma_start(out=taps_sb[:], in_=taps.rearrange("(p t) d -> p (t d)", t=PACK))
+        nc.sync.dma_start(out=taps_sb[:], in_=taps.rearrange("(p t) d -> p (t d)", t=PACK))
         w2_plane = keep.tile([P, N], U8, name="w2_plane", align_bytes=64)
         nc.vector.memset(w2_plane[:].bitcast(I32), 0)
         w2_codes = keep.tile([P, N], U32, name="w2_codes", align_bytes=64)
@@ -79,16 +79,13 @@ def tile_picked_dconv_none_e_kernel(tc, xT, w1, w2_words, w2_scales, taps, offs,
 
         x_codes = [keep.tile([P, T], U32, name=f"x_codes{g}", align_bytes=64) for g in range(PASSES)]
         picked_codes = [keep.tile([P, S], U32, name=f"picked_codes{g}", align_bytes=64) for g in range(PASSES)]
-        picked_scales = []
+        picked_scales = keep.tile([P, S], U8, name="picked_scales", align_bytes=64)
 
-        def pick_scales(half, tag):
-            plane = keep.tile([P, HALF], U8, name=f"picked_scales{half}", tag=tag, align_bytes=64)
-            columns = HALF // 16
-            nc.vector.tensor_copy(out=plane[:], in_=x_scales[:].indirect(offsets[:, columns * half : columns * (half + 1)]))
-            picked_scales.append(plane)
+        def pick_scales():
+            nc.vector.tensor_copy(out=picked_scales[:], in_=x_scales[:].indirect(offsets[:]))
 
         for n, (g, t0, nt, ns) in enumerate(X_PIECES):
-            shares = ((False, ns, nt), (True, 0, ns))
+            shares = [share for share in ((False, ns, nt), (True, 0, ns)) if share[2] > share[1]]
             grouped = [keep.tile([P, PACK * (b - a)], BF16, name=f"x_grouped{n}_{a}", align_bytes=64) for on_scalar, a, b in shares]
             for (on_scalar, a, b), dst in zip(shares, grouped):
                 cast(
@@ -104,25 +101,30 @@ def tile_picked_dconv_none_e_kernel(tc, xT, w1, w2_words, w2_scales, taps, offs,
                 )
             if t0 + nt == T:
                 if g == PASSES - 1:
-                    pick_scales(0, "picked_scales0")
+                    pick_scales()
                 nc.vector.tensor_copy(out=picked_codes[g][:], in_=x_codes[g][:].indirect(offsets[:]))
 
-        h = [[psum.tile([P, HALF], F32, name=f"h{half}_{t}") for t in range(PACK)] for half in range(2)]
+        h = [[psum.tile([P, HALF], F32, name=f"h0_{t}") for t in range(PACK)]]
         w_codes = [keep.tile([P, H], U32, name=f"w_codes{g}", align_bytes=64) for g in range(PASSES)]
         w_scales = [keep.tile([P, H], U8, name=f"w_scales{g}", align_bytes=64) for g in range(PASSES)]
 
-        def cast_w(on_scalar, grouped, base, n, a=0, b=None):
-            g, m0, nm = W_PIECES[n]
-            b = nm if b is None else b
-            cast(
-                on_scalar,
-                grouped[:, :, PACK * (m0 - base + a) : PACK * (m0 - base + b)].rearrange("p t (m j) -> p m j t", j=PACK),
-                w_raw[n][:, :, PACK * a : PACK * b].rearrange("p j (m t) -> p m j t", t=PACK),
-            )
+        def cast_w(n, grouped, base):
+            g, m0, nm, ns = W_PIECES[n]
+            for on_scalar, a, b in ((True, 0, ns), (False, ns, nm)):
+                if b > a:
+                    cast(
+                        on_scalar,
+                        grouped[:, :, PACK * (m0 - base + a) : PACK * (m0 - base + b)].rearrange("p t (m j) -> p m j t", j=PACK),
+                        w_raw[n][:, :, PACK * a : PACK * b].rearrange("p j (m t) -> p m j t", t=PACK),
+                    )
 
-        def quantize_w(g, grouped, base, nm, t):
-            cols = slice(P * t + base, P * t + base + nm)
-            nc.vector.quantize_mx(out=w_codes[g][:, cols].bitcast(FP8X4), scales=w_scales[g][:, cols], in_=grouped[:, t, :])
+        def quantize_w(g, grouped, base, nm, t, count=1):
+            cols = slice(P * t + base, P * (t + count - 1) + base + nm)
+            nc.vector.quantize_mx(
+                out=w_codes[g][:, cols].bitcast(FP8X4),
+                scales=w_scales[g][:, cols],
+                in_=grouped[:, t : t + count, :].rearrange("p t c -> p (t c)"),
+            )
 
         def first_product(g, half, t):
             cols = slice(P * t, P * (t + 1))
@@ -132,31 +134,45 @@ def tile_picked_dconv_none_e_kernel(tc, xT, w1, w2_words, w2_scales, taps, offs,
                 lhsT=w_codes[g][:, cols].bitcast(FP8X4),
                 lhsT_scale=w_scales[g][:, cols],
                 rhs=picked_codes[g][:, entries].bitcast(FP8X4),
-                rhs_scale=picked_scales[half][PACK * g : P, :],
-                start=(g == 0),
-                stop=(g == PASSES - 1),
+                rhs_scale=picked_scales[PACK * g : P, entries],
+                start=(g == half),
+                stop=(g != half),
             )
 
+        for n in range(2):
+            idle = psum.tile([P, S], F32, name=f"warm_up{n}", tag=f"h1_{n}")
+            nc.tensor.matmul_mx(
+                out=idle[:],
+                lhsT=picked_codes[0][:, 0:P].bitcast(FP8X4),
+                lhsT_scale=picked_scales[:, 0:P],
+                rhs=picked_codes[0][:].bitcast(FP8X4),
+                rhs_scale=picked_scales[:],
+                start=True,
+                stop=True,
+            )
+        h.append([psum.tile([P, HALF], F32, name=f"h1_{t}") for t in range(PACK)])
         first = keep.tile([P, PACK, P * PACK], BF16, name="w_first", tag="w_shared", align_bytes=64)
-        cast_w(True, first, 0, 0)
-        cast_w(True, first, 0, 1, 0, 32)
-        cast_w(False, first, 0, 1, 32, 64)
-        for t in range(PACK):
-            quantize_w(0, first, 0, P, t)
-            first_product(0, 0, t)
+        for n, piece in enumerate(W_PIECES):
+            if piece[0] == 0:
+                cast_w(n, first, 0)
+        for t0 in range(0, PACK, 1):
+            quantize_w(0, first, 0, P, t0, 1)
+            for t in range(t0, t0 + 1):
+                first_product(0, 0, t)
         low = keep.tile([P, PACK, 64 * PACK], BF16, name="w_low", align_bytes=64)
         high = keep.tile([P, PACK, 64 * PACK], BF16, name="w_high", tag="w_shared", align_bytes=64)
-        cast_w(True, low, 0, 2)
-        cast_w(False, high, 64, 3)
-        cast_w(True, high, 64, 4, 0, 12)
-        cast_w(False, high, 64, 4, 12, 32)
+        for n, piece in enumerate(W_PIECES):
+            if piece[0] == 1 and piece[1] < 64:
+                cast_w(n, low, 0)
+        for n, piece in enumerate(W_PIECES):
+            if piece[0] == 1 and piece[1] >= 64:
+                cast_w(n, high, 64)
         for t in range(PACK):
             quantize_w(1, low, 0, 64, t)
             quantize_w(1, high, 64, 64, t)
             first_product(1, 0, t)
-        pick_scales(1, "w_shared")
         for t in range(PACK):
-            for g in range(PASSES):
+            for g in (1, 0):
                 first_product(g, 1, t)
 
         def add_tap(half, t, d, count):
@@ -196,15 +212,16 @@ def tile_picked_dconv_none_e_kernel(tc, xT, w1, w2_words, w2_scales, taps, offs,
             z_scales = keep.tile([P, w], U8, name=f"z_scales{n}", align_bytes=64)
             nc.vector.quantize_mx(out=z_codes[:].bitcast(FP8X4), scales=z_scales[:], in_=z[n][:])
             acc = psum.tile([P, w], F32, name=f"acc{n}", tag=f"h0_{n}")
-            nc.tensor.matmul_mx(
-                out=acc[:],
-                lhsT=w2_codes[:].bitcast(FP8X4),
-                lhsT_scale=w2_plane[:],
-                rhs=z_codes[:].bitcast(FP8X4),
-                rhs_scale=z_scales[:],
-                start=True,
-                stop=True,
-            )
+            for e in range(0, w, QUARTER):
+                nc.tensor.matmul_mx(
+                    out=acc[:, e : e + QUARTER],
+                    lhsT=w2_codes[:].bitcast(FP8X4),
+                    lhsT_scale=w2_plane[:],
+                    rhs=z_codes[:, e : e + QUARTER].bitcast(FP8X4),
+                    rhs_scale=z_scales[:, e : e + QUARTER],
+                    start=True,
+                    stop=True,
+                )
             result = keep.tile([P, w], F32, name=f"result{n}")
             nc.scalar.activation(out=result[:], in_=acc[:], func=COPY)
             queue = nc.scalar if n == 2 else nc.sync

@@ -155,12 +155,12 @@ def tile_picked_dconv_none_e_kernel(tc, xT, w1, w2_words, w2_scales, taps, offs,
         for n, piece in enumerate(W_PIECES):
             if piece[0] == 0:
                 cast_w(n, first, 0)
-        for t0 in range(0, PACK, 1):
-            quantize_w(0, first, 0, P, t0, 1)
-            for t in range(t0, t0 + 1):
+        for t0 in range(0, PACK, 4):
+            quantize_w(0, first, 0, P, t0, 4)
+            for t in range(t0, t0 + 4):
                 first_product(0, 0, t)
         low = keep.tile([P, PACK, 64 * PACK], BF16, name="w_low", align_bytes=64)
-        high = keep.tile([P, PACK, 64 * PACK], BF16, name="w_high", tag="w_shared", align_bytes=64)
+        high = keep.tile([P, PACK, 64 * PACK], BF16, name="w_high", align_bytes=64)
         for n, piece in enumerate(W_PIECES):
             if piece[0] == 1 and piece[1] < 64:
                 cast_w(n, low, 0)
@@ -175,12 +175,13 @@ def tile_picked_dconv_none_e_kernel(tc, xT, w1, w2_words, w2_scales, taps, offs,
             for g in (1, 0):
                 first_product(g, 1, t)
 
-        def add_tap(half, t, d, count):
+        def add_tap(half, t, d, count, skip=0):
             first_out = HALF * half + d
-            cols = sums[:, t, first_out : first_out + count]
-            nc.vector.scalar_tensor_tensor(out=cols, in0=h[half][t][:, 0:count], scalar=tap(t, d), in1=cols, op0=MULT, op1=ADD)
+            cols = sums[:, t, first_out + skip : first_out + count]
+            nc.vector.scalar_tensor_tensor(out=cols, in0=h[half][t][:, skip:count], scalar=tap(t, d), in1=cols, op0=MULT, op1=ADD)
 
-        for t in range(PACK):
+        nc.vector.tensor_scalar(out=sums[:, 0, 0:HALF], in0=h[0][0][:], scalar1=tap(0, 0), scalar2=None, op0=MULT)
+        for t in range(1, PACK):
             nc.scalar.activation(out=sums[:, t, 0:HALF], in_=h[0][t][:], func=COPY, scale=tap(t, 0))
         for pair in ((0, 1), (2, 3)):
             for d in (1, 2):
@@ -189,10 +190,12 @@ def tile_picked_dconv_none_e_kernel(tc, xT, w1, w2_words, w2_scales, taps, offs,
         for t in range(PACK):
             nc.scalar.activation(out=sums[:, t, HALF + 2 : S], in_=h[1][t][:, 0 : HALF - 2], func=COPY, scale=tap(t, 2))
             nc.scalar.activation(out=back0[:, t, :], in_=h[1][t][:], func=COPY, scale=tap(t, 0))
-        for t in range(PACK):
+        for t in range(PACK - 1):
             add_tap(1, t, 1, HALF - 1)
+        add_tap(1, PACK - 1, 1, QUARTER - 1)
+        add_tap(1, PACK - 1, 1, HALF - 1, QUARTER - 1)
 
-        chunks = [(0, HALF), (HALF, QUARTER), (HALF + QUARTER, QUARTER)]
+        chunks = [(QUARTER * n, QUARTER) for n in range(4)]
         z = [keep.tile([P, PACK * w], BF16, name=f"z{n}", align_bytes=64) for n, (c0, w) in enumerate(chunks)]
 
         def z_view(n):
@@ -224,12 +227,14 @@ def tile_picked_dconv_none_e_kernel(tc, xT, w1, w2_words, w2_scales, taps, offs,
                 )
             result = keep.tile([P, w], F32, name=f"result{n}")
             nc.scalar.activation(out=result[:], in_=acc[:], func=COPY)
-            queue = nc.scalar if n == 2 else nc.sync
+            queue = nc.scalar if n == 1 else nc.sync
             queue.dma_start(out=out[:, c0 : c0 + w], in_=result[:])
 
-        nc.scalar.activation(out=z_view(0), in_=by_four(sums[:, :, 0:HALF]), func=COPY)
-        back_sum(1)
-        second_product(0)
+        for n in (0, 1):
+            nc.scalar.activation(out=z_view(n), in_=by_four(sums[:, :, QUARTER * n : QUARTER * (n + 1)]), func=COPY)
         back_sum(2)
-        second_product(1)
+        second_product(0)
+        back_sum(3)
         second_product(2)
+        second_product(3)
+        second_product(1)

@@ -22,9 +22,10 @@ K_PASS = P * PACK
 PASSES = K // K_PASS
 
 X_PIECES = [(0, 0, 512, 256), (0, 512, 256, 128), (0, 768, 256, 128), (1, 0, 512, 256), (1, 512, 256, 128), (1, 768, 128, 128), (1, 896, 128, 0)]
-W_PIECES = [(0, 0, 64, 64), (0, 64, 64, 64), (1, 0, 64, 64), (1, 64, 32, 8), (1, 96, 32, 12)]
+W_PIECES = [(0, 0, 64, 64), (0, 64, 64, 56), (1, 0, 64, 64), (1, 64, 32, 0), (1, 96, 32, 12)]
 HALF = S // 2
 QUARTER = S // 4
+EARLY = 384
 
 
 def tile_picked_dconv_none_e_kernel(tc, xT, w1, w2_words, w2_scales, taps, offs, out):
@@ -78,7 +79,8 @@ def tile_picked_dconv_none_e_kernel(tc, xT, w1, w2_words, w2_scales, taps, offs,
             return taps_sb[:, D * t + d : D * t + d + 1]
 
         x_codes = [keep.tile([P, T], U32, name=f"x_codes{g}", align_bytes=64) for g in range(PASSES)]
-        picked_codes = [keep.tile([P, S], U32, name=f"picked_codes{g}", align_bytes=64) for g in range(PASSES)]
+        picked_codes = [keep.tile([P, width], U32, name=f"picked_codes{g}", align_bytes=64) for g, width in enumerate((S, EARLY))]
+        late_codes = []
         picked_scales = keep.tile([P, S], U8, name="picked_scales", align_bytes=64)
 
         def pick_scales():
@@ -102,7 +104,7 @@ def tile_picked_dconv_none_e_kernel(tc, xT, w1, w2_words, w2_scales, taps, offs,
             if t0 + nt == T:
                 if g == PASSES - 1:
                     pick_scales()
-                nc.vector.tensor_copy(out=picked_codes[g][:], in_=x_codes[g][:].indirect(offsets[:]))
+                nc.vector.tensor_copy(out=picked_codes[g][:], in_=x_codes[g][:].indirect(offsets[:, 0 : (S, EARLY)[g] // 16]))
 
         h = [[psum.tile([P, HALF], F32, name=f"h0_{t}") for t in range(PACK)]]
         w_codes = [keep.tile([P, H], U32, name=f"w_codes{g}", align_bytes=64) for g in range(PASSES)]
@@ -126,17 +128,17 @@ def tile_picked_dconv_none_e_kernel(tc, xT, w1, w2_words, w2_scales, taps, offs,
                 in_=grouped[:, t : t + count, :].rearrange("p t c -> p (t c)"),
             )
 
-        def first_product(g, half, t):
+        def first_product(g, t, e0, e1, start, stop):
             cols = slice(P * t, P * (t + 1))
-            entries = slice(HALF * half, HALF * (half + 1))
+            codes = late_codes[0][:, e0 - EARLY : e1 - EARLY] if g == 1 and e0 >= EARLY else picked_codes[g][:, e0:e1]
             nc.tensor.matmul_mx(
-                out=h[half][t][:],
+                out=h[e0 // HALF][t][:, e0 % HALF : e0 % HALF + e1 - e0],
                 lhsT=w_codes[g][:, cols].bitcast(FP8X4),
                 lhsT_scale=w_scales[g][:, cols],
-                rhs=picked_codes[g][:, entries].bitcast(FP8X4),
-                rhs_scale=picked_scales[PACK * g : P, entries],
-                start=(g == half),
-                stop=(g != half),
+                rhs=codes.bitcast(FP8X4),
+                rhs_scale=picked_scales[PACK * g : P, e0:e1],
+                start=start,
+                stop=stop,
             )
 
         for n in range(2):
@@ -158,9 +160,9 @@ def tile_picked_dconv_none_e_kernel(tc, xT, w1, w2_words, w2_scales, taps, offs,
         for t0 in range(0, PACK, 4):
             quantize_w(0, first, 0, P, t0, 4)
             for t in range(t0, t0 + 4):
-                first_product(0, 0, t)
+                first_product(0, t, 0, HALF, True, False)
         low = keep.tile([P, PACK, 64 * PACK], BF16, name="w_low", align_bytes=64)
-        high = keep.tile([P, PACK, 64 * PACK], BF16, name="w_high", align_bytes=64)
+        high = keep.tile([P, PACK, 64 * PACK], BF16, name="w_high", tag="w_high", align_bytes=64)
         for n, piece in enumerate(W_PIECES):
             if piece[0] == 1 and piece[1] < 64:
                 cast_w(n, low, 0)
@@ -170,23 +172,30 @@ def tile_picked_dconv_none_e_kernel(tc, xT, w1, w2_words, w2_scales, taps, offs,
         for t in range(PACK):
             quantize_w(1, low, 0, 64, t)
             quantize_w(1, high, 64, 64, t)
-            first_product(1, 0, t)
+            first_product(1, t, 0, HALF, False, True)
+        late_codes.append(keep.tile([P, S - EARLY], U32, name="late_codes", tag="w_high", align_bytes=64))
+        nc.vector.tensor_copy(out=late_codes[0][:], in_=x_codes[1][:].indirect(offsets[:, EARLY // 16 : S // 16]))
         for t in range(PACK):
-            for g in (1, 0):
-                first_product(g, 1, t)
+            first_product(1, t, HALF, EARLY, True, False)
+            first_product(1, t, EARLY, S, False, False)
+            first_product(0, t, HALF, S, False, True)
 
         def add_tap(half, t, d, count, skip=0):
             first_out = HALF * half + d
             cols = sums[:, t, first_out + skip : first_out + count]
             nc.vector.scalar_tensor_tensor(out=cols, in0=h[half][t][:, skip:count], scalar=tap(t, d), in1=cols, op0=MULT, op1=ADD)
 
-        nc.vector.tensor_scalar(out=sums[:, 0, 0:HALF], in0=h[0][0][:], scalar1=tap(0, 0), scalar2=None, op0=MULT)
+        for a, b in ((0, QUARTER), (QUARTER, HALF)):
+            nc.vector.tensor_scalar(out=sums[:, 0, a:b], in0=h[0][0][:, a:b], scalar1=tap(0, 0), scalar2=None, op0=MULT)
         for t in range(1, PACK):
             nc.scalar.activation(out=sums[:, t, 0:HALF], in_=h[0][t][:], func=COPY, scale=tap(t, 0))
+        add_tap(0, 0, 1, QUARTER - 1)
+        add_tap(0, 0, 1, HALF, QUARTER - 1)
         for pair in ((0, 1), (2, 3)):
             for d in (1, 2):
                 for t in pair:
-                    add_tap(0, t, d, HALF)
+                    if (t, d) != (0, 1):
+                        add_tap(0, t, d, HALF)
         for t in range(PACK):
             nc.scalar.activation(out=sums[:, t, HALF + 2 : S], in_=h[1][t][:, 0 : HALF - 2], func=COPY, scale=tap(t, 2))
             nc.scalar.activation(out=back0[:, t, :], in_=h[1][t][:], func=COPY, scale=tap(t, 0))

@@ -22,10 +22,11 @@ K_PASS = P * PACK
 PASSES = K // K_PASS
 
 X_PIECES = [(0, 0, 512, 256), (0, 512, 256, 128), (0, 768, 256, 128), (1, 0, 512, 256), (1, 512, 256, 128), (1, 768, 128, 128), (1, 896, 128, 0)]
-W_PIECES = [(0, 0, 64, 64), (0, 64, 64, 56), (1, 0, 64, 64), (1, 64, 32, 0), (1, 96, 32, 12)]
+W_PIECES = [(0, 0, 64, 64), (0, 64, 64, 64), (1, 0, 64, 64), (1, 64, 32, 0), (1, 96, 32, 12)]
+W_ON_GPSIMD = (24,)
 HALF = S // 2
 QUARTER = S // 4
-EARLY = 384
+EARLY = 512
 
 
 def tile_picked_dconv_none_e_kernel(tc, xT, w1, w2_words, w2_scales, taps, offs, out):
@@ -112,13 +113,20 @@ def tile_picked_dconv_none_e_kernel(tc, xT, w1, w2_words, w2_scales, taps, offs,
 
         def cast_w(n, grouped, base):
             g, m0, nm, ns = W_PIECES[n]
-            for on_scalar, a, b in ((True, 0, ns), (False, ns, nm)):
-                if b > a:
-                    cast(
-                        on_scalar,
-                        grouped[:, :, PACK * (m0 - base + a) : PACK * (m0 - base + b)].rearrange("p t (m j) -> p m j t", j=PACK),
-                        w_raw[n][:, :, PACK * a : PACK * b].rearrange("p j (m t) -> p m j t", t=PACK),
-                    )
+            shares = [("scalar", ns), ("vector", nm - ns)]
+            if n == 1:
+                shares = [("gpsimd", count) for count in W_ON_GPSIMD] + [("scalar", nm - sum(W_ON_GPSIMD))]
+            a = 0
+            for engine, count in shares:
+                b = a + count
+                if count:
+                    dst = grouped[:, :, PACK * (m0 - base + a) : PACK * (m0 - base + b)].rearrange("p t (m j) -> p m j t", j=PACK)
+                    src = w_raw[n][:, :, PACK * a : PACK * b].rearrange("p j (m t) -> p m j t", t=PACK)
+                    if engine == "gpsimd":
+                        nc.gpsimd.tensor_scalar(out=dst.rearrange("p m j t -> p t m j"), in0=src.rearrange("p m j t -> p t m j"), scalar1=1.0, scalar2=0.0, op0=MULT, op1=ADD)
+                    else:
+                        cast(engine == "scalar", dst, src)
+                a = b
 
         def quantize_w(g, grouped, base, nm, t, count=1):
             cols = slice(P * t + base, P * (t + count - 1) + base + nm)
@@ -173,11 +181,8 @@ def tile_picked_dconv_none_e_kernel(tc, xT, w1, w2_words, w2_scales, taps, offs,
             quantize_w(1, low, 0, 64, t)
             quantize_w(1, high, 64, 64, t)
             first_product(1, t, 0, HALF, False, True)
-        late_codes.append(keep.tile([P, S - EARLY], U32, name="late_codes", tag="w_high", align_bytes=64))
-        nc.vector.tensor_copy(out=late_codes[0][:], in_=x_codes[1][:].indirect(offsets[:, EARLY // 16 : S // 16]))
         for t in range(PACK):
-            first_product(1, t, HALF, EARLY, True, False)
-            first_product(1, t, EARLY, S, False, False)
+            first_product(1, t, HALF, S, True, False)
             first_product(0, t, HALF, S, False, True)
 
         def add_tap(half, t, d, count, skip=0):

@@ -149,17 +149,6 @@ def tile_picked_dconv_none_e_kernel(tc, xT, w1, w2_words, w2_scales, taps, offs,
                 stop=stop,
             )
 
-        for n in range(2):
-            idle = psum.tile([P, S], F32, name=f"warm_up{n}", tag=f"h1_{n}")
-            nc.tensor.matmul_mx(
-                out=idle[:],
-                lhsT=picked_codes[0][:, 0:P].bitcast(FP8X4),
-                lhsT_scale=picked_scales[:, 0:P],
-                rhs=picked_codes[0][:].bitcast(FP8X4),
-                rhs_scale=picked_scales[:],
-                start=True,
-                stop=True,
-            )
         h.append([psum.tile([P, HALF], F32, name=f"h1_{t}") for t in range(PACK)])
         first = keep.tile([P, PACK, P * PACK], BF16, name="w_first", tag="w_shared", align_bytes=64)
         for n, piece in enumerate(W_PIECES):

@@ -154,9 +154,9 @@ def tile_picked_dconv_none_e_kernel(tc, xT, w1, w2_words, w2_scales, taps, offs,
         for n, piece in enumerate(W_PIECES):
             if piece[0] == 0:
                 cast_w(n, first, 0)
-        for t0 in range(0, PACK, 4):
-            quantize_w(0, first, 0, P, t0, 4)
-            for t in range(t0, t0 + 4):
+        for t0, count in ((0, 1), (1, 1), (2, 2)):
+            quantize_w(0, first, 0, P, t0, count)
+            for t in range(t0, t0 + count):
                 first_product(0, t, 0, HALF, True, False)
         low = keep.tile([P, PACK, 64 * PACK], BF16, name="w_low", align_bytes=64)
         high = keep.tile([P, PACK, 64 * PACK], BF16, name="w_high", tag="w_high", align_bytes=64)

@@ -124,8 +124,10 @@ def tile_picked_dconv_none_e_kernel(tc, xT, w1, w2_words, w2_scales, taps, offs,
                     src = w_raw[n][:, :, PACK * a : PACK * b].rearrange("p j (m t) -> p m j t", t=PACK)
                     if engine == "gpsimd":
                         nc.gpsimd.tensor_scalar(out=dst.rearrange("p m j t -> p t m j"), in0=src.rearrange("p m j t -> p t m j"), scalar1=1.0, scalar2=0.0, op0=MULT, op1=ADD)
+                    elif engine == "vector":
+                        cast(False, dst.rearrange("p m j t -> p m t j"), src.rearrange("p m j t -> p m t j"))
                     else:
-                        cast(engine == "scalar", dst, src)
+                        cast(True, dst, src)
                 a = b
 
         def quantize_w(g, grouped, base, nm, t, count=1):

@@ -40,6 +40,7 @@ def tile_picked_dconv_none_e_kernel(tc, xT, w1, w2_words, w2_scales, taps, offs,
 
     with ExitStack() as ctx:
         keep = ctx.enter_context(tc.tile_pool(name="keep", bufs=1))
+        reuse = ctx.enter_context(tc.tile_pool(name="reuse", bufs=1))
         psum = ctx.enter_context(tc.psum_pool(name="psum", bufs=1))
 
         offsets = keep.tile([P, S // 16], U16, name="offsets")
@@ -72,12 +73,10 @@ def tile_picked_dconv_none_e_kernel(tc, xT, w1, w2_words, w2_scales, taps, offs,
                 in_=w2_scales[0, 4 * q : 4 * q + 4, :].bitcast(I32),
             )
 
-        sums = keep.tile([P, PACK, S], F32, name="sums")
-        back0 = keep.tile([P, PACK, HALF], F32, name="back0")
-        nc.vector.memset(sums[:, :, HALF : HALF + 2], 0.0)
-
-        def tap(t, d):
-            return taps_sb[:, D * t + d : D * t + d + 1]
+        sums = reuse.tile([P, PACK, S], F32, name="sums", offset=0, align_bytes=64)
+        back = keep.tile([P, PACK, HALF], F32, name="back")
+        near = keep.tile([P, PACK, HALF], F32, name="near")
+        nc.vector.memset(sums[:, :, 0:2], 0.0)
 
         x_codes = [keep.tile([P, T], U32, name=f"x_codes{g}", align_bytes=64) for g in range(PASSES)]
         picked_codes = [keep.tile([P, width], U32, name=f"picked_codes{g}", align_bytes=64) for g, width in enumerate((S, EARLY))]
@@ -176,70 +175,87 @@ def tile_picked_dconv_none_e_kernel(tc, xT, w1, w2_words, w2_scales, taps, offs,
             first_product(1, t, HALF, S, True, False)
             first_product(0, t, HALF, S, False, True)
 
-        def add_tap(half, t, d, count, skip=0):
-            first_out = HALF * half + d
-            cols = sums[:, t, first_out + skip : first_out + count]
-            nc.vector.scalar_tensor_tensor(out=cols, in0=h[half][t][:, skip:count], scalar=tap(t, d), in1=cols, op0=MULT, op1=ADD)
+        def tap(t, d):
+            return taps_sb[:, D * t + d : D * t + d + 1]
 
-        for a, b in ((0, QUARTER), (QUARTER, HALF)):
-            nc.vector.tensor_scalar(out=sums[:, 0, a:b], in0=h[0][0][:, a:b], scalar1=tap(0, 0), scalar2=None, op0=MULT)
-        for t in range(1, PACK):
-            nc.scalar.activation(out=sums[:, t, 0:HALF], in_=h[0][t][:], func=COPY, scale=tap(t, 0))
-        add_tap(0, 0, 1, QUARTER - 1)
-        add_tap(0, 0, 1, HALF, QUARTER - 1)
-        for pair in ((0, 1), (2, 3)):
-            for d in (1, 2):
-                for t in pair:
-                    if (t, d) != (0, 1):
-                        add_tap(0, t, d, HALF)
-        for t in range(PACK):
-            nc.scalar.activation(out=sums[:, t, HALF + 2 : S], in_=h[1][t][:, 0 : HALF - 2], func=COPY, scale=tap(t, 2))
-            nc.scalar.activation(out=back0[:, t, :], in_=h[1][t][:], func=COPY, scale=tap(t, 0))
-        for t in range(PACK - 1):
-            add_tap(1, t, 1, HALF - 1)
-        add_tap(1, PACK - 1, 1, QUARTER - 1)
-        add_tap(1, PACK - 1, 1, HALF - 1, QUARTER - 1)
+        def term(on_scalar, dst, src, t, d):
+            if on_scalar:
+                nc.scalar.activation(out=dst, in_=src, func=COPY, scale=tap(t, d))
+            else:
+                nc.vector.tensor_scalar(out=dst, in0=src, scalar1=tap(t, d), scalar2=None, op0=MULT)
 
-        chunks = [(QUARTER * n, QUARTER) for n in range(4)]
-        z = [keep.tile([P, PACK * w], BF16, name=f"z{n}", align_bytes=64) for n, (c0, w) in enumerate(chunks)]
+        def h_cols(q, t, d):
+            a = QUARTER * (q % 2)
+            count = min(QUARTER, S - d - QUARTER * q)
+            return h[q // 2][t][:, a : a + count], slice(QUARTER * q + d, QUARTER * q + d + count)
 
-        def z_view(n):
-            return z[n][:].rearrange("p (c i t) -> p c t i", i=4, t=PACK)
+        def far_term(on_scalar, q, t):
+            src, cols = h_cols(q, t, 2)
+            term(on_scalar, sums[:, t, cols], src, t, 2)
 
-        def by_four(ap):
-            return ap.rearrange("p t (c i) -> p c t i", i=4)
+        def near_term(on_scalar, q, t):
+            src, cols = h_cols(q, t, 0)
+            term(on_scalar, near[:, t, cols], src, t, 0)
 
-        def back_sum(n):
-            c0, w = chunks[n]
-            cols = slice(c0 - HALF, c0 - HALF + w)
-            nc.vector.tensor_tensor(out=z_view(n), in0=by_four(sums[:, :, c0 : c0 + w]), in1=by_four(back0[:, :, cols]), op=ADD)
+        def add_tap(q, t, d):
+            src, cols = h_cols(q, t, d)
+            dst = sums[:, t, cols] if d else back[:, t, cols.start - HALF : cols.stop - HALF]
+            nc.vector.scalar_tensor_tensor(out=dst, in0=src, scalar=tap(t, d), in1=sums[:, t, cols], op0=MULT, op1=ADD)
 
-        def second_product(n):
-            c0, w = chunks[n]
-            z_codes = keep.tile([P, w], U32, name=f"z_codes{n}", align_bytes=64)
-            z_scales = keep.tile([P, w], U8, name=f"z_scales{n}", align_bytes=64)
-            nc.vector.quantize_mx(out=z_codes[:].bitcast(FP8X4), scales=z_scales[:], in_=z[n][:])
-            acc = psum.tile([P, w], F32, name=f"acc{n}", tag=f"h0_{n}")
-            for e in range(0, w, QUARTER):
-                nc.tensor.matmul_mx(
-                    out=acc[:, e : e + QUARTER],
-                    lhsT=w2_codes[:].bitcast(FP8X4),
-                    lhsT_scale=w2_plane[:],
-                    rhs=z_codes[:, e : e + QUARTER].bitcast(FP8X4),
-                    rhs_scale=z_scales[:, e : e + QUARTER],
-                    start=True,
-                    stop=True,
-                )
-            result = keep.tile([P, w], F32, name=f"result{n}")
+        z = [keep.tile([P, PACK * QUARTER], BF16, name=f"z{q}", align_bytes=64) for q in range(4)]
+
+        def close_on_gpsimd(q):
+            cols = slice(QUARTER * q, QUARTER * (q + 1))
+            nc.gpsimd.tensor_tensor(
+                out=z[q][:].rearrange("p (c i t) -> p c t i", i=4, t=PACK),
+                in0=sums[:, :, cols].rearrange("p t (c i) -> p c t i", i=4),
+                in1=near[:, :, cols].rearrange("p t (c i) -> p c t i", i=4),
+                op=ADD,
+            )
+
+        def close_on_scalar(q):
+            nc.scalar.activation(
+                out=z[q][:].rearrange("p (c i t) -> p c t i", i=4, t=PACK),
+                in_=back[:, :, QUARTER * q - HALF : QUARTER * (q + 1) - HALF].rearrange("p t (c i) -> p c t i", i=4),
+                func=COPY,
+            )
+
+        def second_product(q):
+            z_codes = reuse.tile([P, QUARTER], U32, name=f"z_codes{q}", offset=4 * QUARTER * q, align_bytes=64)
+            z_scales = keep.tile([P, QUARTER], U8, name=f"z_scales{q}", align_bytes=64)
+            nc.vector.quantize_mx(out=z_codes[:].bitcast(FP8X4), scales=z_scales[:], in_=z[q][:])
+            acc = psum.tile([P, QUARTER], F32, name=f"acc{q}", tag=f"h0_{q}")
+            nc.tensor.matmul_mx(
+                out=acc[:],
+                lhsT=w2_codes[:].bitcast(FP8X4),
+                lhsT_scale=w2_plane[:],
+                rhs=z_codes[:].bitcast(FP8X4),
+                rhs_scale=z_scales[:],
+                start=True,
+                stop=True,
+            )
+            result = keep.tile([P, QUARTER], F32, name=f"result{q}")
             nc.scalar.activation(out=result[:], in_=acc[:], func=COPY)
-            queue = nc.scalar if n == 1 else nc.sync
-            queue.dma_start(out=out[:, c0 : c0 + w], in_=result[:])
+            nc.sync.dma_start(out=out[:, QUARTER * q : QUARTER * (q + 1)], in_=result[:])
 
-        for n in (0, 1):
-            nc.scalar.activation(out=z_view(n), in_=by_four(sums[:, :, QUARTER * n : QUARTER * (n + 1)]), func=COPY)
-        back_sum(2)
-        second_product(0)
-        back_sum(3)
-        second_product(2)
-        second_product(3)
-        second_product(1)
+        for t in range(PACK):
+            far_term(t > 0, 0, t)
+            near_term(t > 0, 0, t)
+            add_tap(0, t, 1)
+        close_on_gpsimd(0)
+        for t in range(PACK):
+            far_term(t == PACK - 1, 1, t)
+        for t in range(PACK):
+            add_tap(1, t, 1)
+        for t in range(PACK):
+            near_term(True, 1, t)
+        close_on_gpsimd(1)
+        for t in range(PACK):
+            term(True, sums[:, t, HALF + 2 : S], h[1][t][:, 0 : HALF - 2], t, 2)
+        for q in (2, 3):
+            for d in (1, 0):
+                for t in range(PACK):
+                    add_tap(q, t, d)
+            close_on_scalar(q)
+        for q in range(4):
+            second_product(q)

@@ -27,6 +27,8 @@ W_ON_GPSIMD = (24,)
 HALF = S // 2
 QUARTER = S // 4
 EARLY = 512
+NEAR_BYTES = 4 * PACK * HALF
+LAST = 64
 
 
 def tile_picked_dconv_none_e_kernel(tc, xT, w1, w2_words, w2_scales, taps, offs, out):
@@ -73,9 +75,9 @@ def tile_picked_dconv_none_e_kernel(tc, xT, w1, w2_words, w2_scales, taps, offs,
                 in_=w2_scales[0, 4 * q : 4 * q + 4, :].bitcast(I32),
             )
 
-        sums = reuse.tile([P, PACK, S], F32, name="sums", offset=0, align_bytes=64)
-        back = keep.tile([P, PACK, HALF], F32, name="back")
-        near = keep.tile([P, PACK, HALF], F32, name="near")
+        sums = keep.tile([P, PACK, S], F32, name="sums")
+        near = reuse.tile([P, PACK, HALF], F32, name="near", offset=0, align_bytes=64)
+        last_tap = reuse.tile([P, 1], F32, name="last_tap", offset=NEAR_BYTES, align_bytes=64)
         nc.vector.memset(sums[:, :, 0:2], 0.0)
 
         x_codes = [keep.tile([P, T], U32, name=f"x_codes{g}", align_bytes=64) for g in range(PASSES)]
@@ -141,7 +143,7 @@ def tile_picked_dconv_none_e_kernel(tc, xT, w1, w2_words, w2_scales, taps, offs,
             cols = slice(P * t, P * (t + 1))
             codes = late_codes[0][:, e0 - EARLY : e1 - EARLY] if g == 1 and e0 >= EARLY else picked_codes[g][:, e0:e1]
             nc.tensor.matmul_mx(
-                out=h[e0 // HALF][t][:, e0 % HALF : e0 % HALF + e1 - e0],
+                out=h[0][t][:, e0:e1] if e0 < HALF else back_h(e0 // QUARTER, t),
                 lhsT=w_codes[g][:, cols].bitcast(FP8X4),
                 lhsT_scale=w_scales[g][:, cols],
                 rhs=codes.bitcast(FP8X4),
@@ -150,7 +152,11 @@ def tile_picked_dconv_none_e_kernel(tc, xT, w1, w2_words, w2_scales, taps, offs,
                 stop=stop,
             )
 
-        h.append([psum.tile([P, HALF], F32, name=f"h1_{t}") for t in range(PACK)])
+        back_banks = [[psum.tile([P, 2, QUARTER], F32, name=f"h{q}_pair{u}") for u in range(2)] for q in (2, 3)]
+
+        def back_h(q, t):
+            return back_banks[q - 2][t // 2][:, t % 2, :]
+
         first = keep.tile([P, PACK, P * PACK], BF16, name="w_first", tag="w_shared", align_bytes=64)
         for n, piece in enumerate(W_PIECES):
             if piece[0] == 0:
@@ -171,9 +177,10 @@ def tile_picked_dconv_none_e_kernel(tc, xT, w1, w2_words, w2_scales, taps, offs,
             quantize_w(1, low, 0, 64, t)
             quantize_w(1, high, 64, 64, t)
             first_product(1, t, 0, HALF, False, True)
-        for t in range(PACK):
-            first_product(1, t, HALF, S, True, False)
-            first_product(0, t, HALF, S, False, True)
+        for q in (2, 3):
+            for t in range(PACK):
+                first_product(1, t, QUARTER * q, QUARTER * (q + 1), True, False)
+                first_product(0, t, QUARTER * q, QUARTER * (q + 1), False, True)
 
         def tap(t, d):
             return taps_sb[:, D * t + d : D * t + d + 1]
@@ -187,7 +194,8 @@ def tile_picked_dconv_none_e_kernel(tc, xT, w1, w2_words, w2_scales, taps, offs,
         def h_cols(q, t, d):
             a = QUARTER * (q % 2)
             count = min(QUARTER, S - d - QUARTER * q)
-            return h[q // 2][t][:, a : a + count], slice(QUARTER * q + d, QUARTER * q + d + count)
+            src = h[0][t][:, a : a + count] if q < 2 else back_h(q, t)[:, 0:count]
+            return src, slice(QUARTER * q + d, QUARTER * q + d + count)
 
         def far_term(on_scalar, q, t):
             src, cols = h_cols(q, t, 2)
@@ -197,10 +205,15 @@ def tile_picked_dconv_none_e_kernel(tc, xT, w1, w2_words, w2_scales, taps, offs,
             src, cols = h_cols(q, t, 0)
             term(on_scalar, near[:, t, cols], src, t, 0)
 
+        nc.scalar.copy(out=last_tap[:], in_=tap(0, 0))
+
         def add_tap(q, t, d):
             src, cols = h_cols(q, t, d)
-            dst = sums[:, t, cols] if d else back[:, t, cols.start - HALF : cols.stop - HALF]
-            nc.vector.scalar_tensor_tensor(out=dst, in0=src, scalar=tap(t, d), in1=sums[:, t, cols], op0=MULT, op1=ADD)
+            nc.vector.scalar_tensor_tensor(out=sums[:, t, cols], in0=src, scalar=tap(t, d), in1=sums[:, t, cols], op0=MULT, op1=ADD)
+
+        def add_near(t, a, b, scalar):
+            cols = sums[:, t, 3 * QUARTER + a : 3 * QUARTER + b]
+            nc.vector.scalar_tensor_tensor(out=cols, in0=back_h(3, t)[:, a:b], scalar=scalar, in1=cols, op0=MULT, op1=ADD)
 
         z = [keep.tile([P, PACK * QUARTER], BF16, name=f"z{q}", align_bytes=64) for q in range(4)]
 
@@ -213,49 +226,64 @@ def tile_picked_dconv_none_e_kernel(tc, xT, w1, w2_words, w2_scales, taps, offs,
                 op=ADD,
             )
 
-        def close_on_scalar(q):
+        def close_on_scalar(q, a, b):
             nc.scalar.activation(
-                out=z[q][:].rearrange("p (c i t) -> p c t i", i=4, t=PACK),
-                in_=back[:, :, QUARTER * q - HALF : QUARTER * (q + 1) - HALF].rearrange("p t (c i) -> p c t i", i=4),
+                out=z[q][:, PACK * a : PACK * b].rearrange("p (c i t) -> p c t i", i=4, t=PACK),
+                in_=sums[:, :, QUARTER * q + a : QUARTER * q + b].rearrange("p t (c i) -> p c t i", i=4),
                 func=COPY,
             )
 
+        all_codes = reuse.tile([P, S], U32, name="z_codes", offset=NEAR_BYTES + 64 - 4 * S, align_bytes=64)
+
         def second_product(q):
-            z_codes = reuse.tile([P, QUARTER], U32, name=f"z_codes{q}", offset=4 * QUARTER * q, align_bytes=64)
+            z_codes = all_codes[:, QUARTER * q : QUARTER * (q + 1)]
             z_scales = keep.tile([P, QUARTER], U8, name=f"z_scales{q}", align_bytes=64)
-            nc.vector.quantize_mx(out=z_codes[:].bitcast(FP8X4), scales=z_scales[:], in_=z[q][:])
+            nc.vector.quantize_mx(out=z_codes.bitcast(FP8X4), scales=z_scales[:], in_=z[q][:])
             acc = psum.tile([P, QUARTER], F32, name=f"acc{q}", tag=f"h0_{q}")
             nc.tensor.matmul_mx(
                 out=acc[:],
                 lhsT=w2_codes[:].bitcast(FP8X4),
                 lhsT_scale=w2_plane[:],
-                rhs=z_codes[:].bitcast(FP8X4),
+                rhs=z_codes.bitcast(FP8X4),
                 rhs_scale=z_scales[:],
                 start=True,
                 stop=True,
             )
             result = keep.tile([P, QUARTER], F32, name=f"result{q}")
             nc.scalar.activation(out=result[:], in_=acc[:], func=COPY)
-            nc.sync.dma_start(out=out[:, QUARTER * q : QUARTER * (q + 1)], in_=result[:])
+            queue = nc.scalar if q == 3 else nc.sync
+            queue.dma_start(out=out[:, QUARTER * q : QUARTER * (q + 1)], in_=result[:])
 
         for t in range(PACK):
             far_term(t > 0, 0, t)
-            near_term(t > 0, 0, t)
+            if t != 1:
+                near_term(t > 0, 0, t)
             add_tap(0, t, 1)
+            if t == 1:
+                near_term(False, 0, t)
         close_on_gpsimd(0)
         for t in range(PACK):
-            far_term(t == PACK - 1, 1, t)
+            far_term(t in (1, 2), 1, t)
         for t in range(PACK):
             add_tap(1, t, 1)
-        for t in range(PACK):
+        for u in range(2):
+            near_term(True, 1, u)
+            for t in (2 * u, 2 * u + 1):
+                far_term(True, 2, t)
+        for t in (2, 3):
             near_term(True, 1, t)
         close_on_gpsimd(1)
+        for d in (1, 0):
+            for t in range(PACK):
+                add_tap(2, t, d)
         for t in range(PACK):
-            term(True, sums[:, t, HALF + 2 : S], h[1][t][:, 0 : HALF - 2], t, 2)
-        for q in (2, 3):
-            for d in (1, 0):
-                for t in range(PACK):
-                    add_tap(q, t, d)
-            close_on_scalar(q)
+            far_term(True, 3, t)
+        close_on_scalar(2, 0, QUARTER)
+        for t in range(PACK):
+            add_tap(3, t, 1)
+        for a, b in ((0, QUARTER - LAST), (QUARTER - LAST, QUARTER)):
+            for t in range(PACK):
+                add_near(t, a, b, last_tap[:] if a and t == 0 else tap(t, 0))
+            close_on_scalar(3, a, b)
         for q in range(4):
             second_product(q)

@@ -26,7 +26,6 @@ W_PIECES = [(0, 0, 64, 64), (0, 64, 64, 64), (1, 0, 64, 64), (1, 64, 32, 0), (1,
 W_ON_GPSIMD = (24,)
 HALF = S // 2
 QUARTER = S // 4
-EARLY = 512
 NEAR_BYTES = 4 * PACK * HALF
 LAST = 64
 
@@ -81,8 +80,7 @@ def tile_picked_dconv_none_e_kernel(tc, xT, w1, w2_words, w2_scales, taps, offs,
         nc.vector.memset(sums[:, :, 0:2], 0.0)
 
         x_codes = [keep.tile([P, T], U32, name=f"x_codes{g}", align_bytes=64) for g in range(PASSES)]
-        picked_codes = [keep.tile([P, width], U32, name=f"picked_codes{g}", align_bytes=64) for g, width in enumerate((S, EARLY))]
-        late_codes = []
+        picked_codes = [keep.tile([P, S], U32, name=f"picked_codes{g}", align_bytes=64) for g in range(PASSES)]
         picked_scales = keep.tile([P, S], U8, name="picked_scales", align_bytes=64)
 
         def pick_scales():
@@ -106,9 +104,8 @@ def tile_picked_dconv_none_e_kernel(tc, xT, w1, w2_words, w2_scales, taps, offs,
             if t0 + nt == T:
                 if g == PASSES - 1:
                     pick_scales()
-                nc.vector.tensor_copy(out=picked_codes[g][:], in_=x_codes[g][:].indirect(offsets[:, 0 : (S, EARLY)[g] // 16]))
+                nc.vector.tensor_copy(out=picked_codes[g][:], in_=x_codes[g][:].indirect(offsets[:]))
 
-        h = [[psum.tile([P, HALF], F32, name=f"h0_{t}") for t in range(PACK)]]
         w_codes = [keep.tile([P, H], U32, name=f"w_codes{g}", align_bytes=64) for g in range(PASSES)]
         w_scales = [keep.tile([P, H], U8, name=f"w_scales{g}", align_bytes=64) for g in range(PASSES)]
 
@@ -139,24 +136,27 @@ def tile_picked_dconv_none_e_kernel(tc, xT, w1, w2_words, w2_scales, taps, offs,
                 in_=grouped[:, t : t + count, :].rearrange("p t c -> p (t c)"),
             )
 
-        def first_product(g, t, e0, e1, start, stop):
+        h = [[psum.tile([P, QUARTER], F32, name=f"h0_{t}", tag=f"bank{t}")[:] for t in range(PACK)]]
+
+        def open_quarter(q):
+            banks = [psum.tile([P, 2, QUARTER], F32, name=f"h{q}_pair{u}", tag=f"bank{(2 * q + 2 + u) % 8}") for u in range(2)]
+            h.append([banks[t // 2][:, t % 2, :] for t in range(PACK)])
+
+        def first_product(g, q, t, start, stop):
             cols = slice(P * t, P * (t + 1))
-            codes = late_codes[0][:, e0 - EARLY : e1 - EARLY] if g == 1 and e0 >= EARLY else picked_codes[g][:, e0:e1]
+            entries = slice(QUARTER * q, QUARTER * (q + 1))
             nc.tensor.matmul_mx(
-                out=h[0][t][:, e0:e1] if e0 < HALF else back_h(e0 // QUARTER, t),
+                out=h[q][t],
                 lhsT=w_codes[g][:, cols].bitcast(FP8X4),
                 lhsT_scale=w_scales[g][:, cols],
-                rhs=codes.bitcast(FP8X4),
-                rhs_scale=picked_scales[PACK * g : P, e0:e1],
+                rhs=picked_codes[g][:, entries].bitcast(FP8X4),
+                rhs_scale=picked_scales[PACK * g : P, entries],
                 start=start,
                 stop=stop,
             )
 
-        back_banks = [[psum.tile([P, 2, QUARTER], F32, name=f"h{q}_pair{u}") for u in range(2)] for q in (2, 3)]
-
-        def back_h(q, t):
-            return back_banks[q - 2][t // 2][:, t % 2, :]
-
+        open_quarter(1)
+        open_quarter(2)
         first = keep.tile([P, PACK, P * PACK], BF16, name="w_first", tag="w_shared", align_bytes=64)
         for n, piece in enumerate(W_PIECES):
             if piece[0] == 0:
@@ -164,7 +164,8 @@ def tile_picked_dconv_none_e_kernel(tc, xT, w1, w2_words, w2_scales, taps, offs,
         for t0, count in ((0, 1), (1, 1), (2, 2)):
             quantize_w(0, first, 0, P, t0, count)
             for t in range(t0, t0 + count):
-                first_product(0, t, 0, HALF, True, False)
+                first_product(0, 0, t, True, False)
+                first_product(0, 1, t, t % 2 == 0, False)
         low = keep.tile([P, PACK, 64 * PACK], BF16, name="w_low", align_bytes=64)
         high = keep.tile([P, PACK, 64 * PACK], BF16, name="w_high", tag="w_high", align_bytes=64)
         for n, piece in enumerate(W_PIECES):
@@ -176,11 +177,16 @@ def tile_picked_dconv_none_e_kernel(tc, xT, w1, w2_words, w2_scales, taps, offs,
         for t in range(PACK):
             quantize_w(1, low, 0, 64, t)
             quantize_w(1, high, 64, 64, t)
-            first_product(1, t, 0, HALF, False, True)
-        for q in (2, 3):
-            for t in range(PACK):
-                first_product(1, t, QUARTER * q, QUARTER * (q + 1), True, False)
-                first_product(0, t, QUARTER * q, QUARTER * (q + 1), False, True)
+            first_product(1, 0, t, False, True)
+        for t in range(PACK):
+            first_product(1, 1, t, False, t % 2 == 1)
+
+        def back_products(q, tiles):
+            for t in tiles:
+                first_product(1, q, t, True, False)
+                first_product(0, q, t, False, True)
+
+        back_products(2, range(PACK))
 
         def tap(t, d):
             return taps_sb[:, D * t + d : D * t + d + 1]
@@ -192,10 +198,8 @@ def tile_picked_dconv_none_e_kernel(tc, xT, w1, w2_words, w2_scales, taps, offs,
                 nc.vector.tensor_scalar(out=dst, in0=src, scalar1=tap(t, d), scalar2=None, op0=MULT)
 
         def h_cols(q, t, d):
-            a = QUARTER * (q % 2)
             count = min(QUARTER, S - d - QUARTER * q)
-            src = h[0][t][:, a : a + count] if q < 2 else back_h(q, t)[:, 0:count]
-            return src, slice(QUARTER * q + d, QUARTER * q + d + count)
+            return h[q][t][:, 0:count], slice(QUARTER * q + d, QUARTER * q + d + count)
 
         def far_term(on_scalar, q, t):
             src, cols = h_cols(q, t, 2)
@@ -213,7 +217,7 @@ def tile_picked_dconv_none_e_kernel(tc, xT, w1, w2_words, w2_scales, taps, offs,
 
         def add_near(t, a, b, scalar):
             cols = sums[:, t, 3 * QUARTER + a : 3 * QUARTER + b]
-            nc.vector.scalar_tensor_tensor(out=cols, in0=back_h(3, t)[:, a:b], scalar=scalar, in1=cols, op0=MULT, op1=ADD)
+            nc.vector.scalar_tensor_tensor(out=cols, in0=h[3][t][:, a:b], scalar=scalar, in1=cols, op0=MULT, op1=ADD)
 
         z = [keep.tile([P, PACK * QUARTER], BF16, name=f"z{q}", align_bytes=64) for q in range(4)]
 
@@ -239,7 +243,7 @@ def tile_picked_dconv_none_e_kernel(tc, xT, w1, w2_words, w2_scales, taps, offs,
             z_codes = all_codes[:, QUARTER * q : QUARTER * (q + 1)]
             z_scales = keep.tile([P, QUARTER], U8, name=f"z_scales{q}", align_bytes=64)
             nc.vector.quantize_mx(out=z_codes.bitcast(FP8X4), scales=z_scales[:], in_=z[q][:])
-            acc = psum.tile([P, QUARTER], F32, name=f"acc{q}", tag=f"h0_{q}")
+            acc = psum.tile([P, QUARTER], F32, name=f"acc{q}", tag=f"bank{2 + q}")
             nc.tensor.matmul_mx(
                 out=acc[:],
                 lhsT=w2_codes[:].bitcast(FP8X4),
@@ -254,25 +258,28 @@ def tile_picked_dconv_none_e_kernel(tc, xT, w1, w2_words, w2_scales, taps, offs,
             queue = nc.scalar if q == 3 else nc.sync
             queue.dma_start(out=out[:, QUARTER * q : QUARTER * (q + 1)], in_=result[:])
 
+        far_term(False, 0, 0)
+        near_term(False, 0, 0)
         for t in range(PACK):
-            far_term(t > 0, 0, t)
-            if t != 1:
-                near_term(t > 0, 0, t)
+            if t:
+                far_term(True, 0, t)
             add_tap(0, t, 1)
-            if t == 1:
-                near_term(False, 0, t)
+        for t in range(1, PACK):
+            near_term(t < PACK - 1, 0, t)
         close_on_gpsimd(0)
+        open_quarter(3)
+        back_products(3, range(PACK))
         for t in range(PACK):
-            far_term(t in (1, 2), 1, t)
+            far_term(t >= 2, 1, t)
         for t in range(PACK):
             add_tap(1, t, 1)
-        for u in range(2):
-            near_term(True, 1, u)
-            for t in (2 * u, 2 * u + 1):
-                far_term(True, 2, t)
-        for t in (2, 3):
+        for t in (0, 1):
+            far_term(True, 2, t)
+        for t in range(PACK):
             near_term(True, 1, t)
         close_on_gpsimd(1)
+        for t in (2, 3):
+            far_term(True, 2, t)
         for d in (1, 0):
             for t in range(PACK):
                 add_tap(2, t, d)

@@ -28,6 +28,7 @@ HALF = S // 2
 QUARTER = S // 4
 NEAR_BYTES = 4 * PACK * HALF
 LAST = 64
+SECOND = 88
 
 
 def tile_picked_dconv_none_e_kernel(tc, xT, w1, w2_words, w2_scales, taps, offs, out):
@@ -206,8 +207,8 @@ def tile_picked_dconv_none_e_kernel(tc, xT, w1, w2_words, w2_scales, taps, offs,
             term(on_scalar, sums[:, t, cols], src, t, 2)
 
         def near_term(on_scalar, q, t):
-            src, cols = h_cols(q, t, 0)
-            term(on_scalar, near[:, t, cols], src, t, 0)
+            count = SECOND if q else QUARTER
+            term(on_scalar, near[:, t, QUARTER * q : QUARTER * q + count], h[q][t][:, 0:count], t, 0)
 
         nc.scalar.copy(out=last_tap[:], in_=tap(0, 0))
 
@@ -215,25 +216,25 @@ def tile_picked_dconv_none_e_kernel(tc, xT, w1, w2_words, w2_scales, taps, offs,
             src, cols = h_cols(q, t, d)
             nc.vector.scalar_tensor_tensor(out=sums[:, t, cols], in0=src, scalar=tap(t, d), in1=sums[:, t, cols], op0=MULT, op1=ADD)
 
-        def add_near(t, a, b, scalar):
-            cols = sums[:, t, 3 * QUARTER + a : 3 * QUARTER + b]
-            nc.vector.scalar_tensor_tensor(out=cols, in0=h[3][t][:, a:b], scalar=scalar, in1=cols, op0=MULT, op1=ADD)
+        def add_near(q, t, a, b, scalar):
+            cols = sums[:, t, QUARTER * q + a : QUARTER * q + b]
+            nc.vector.scalar_tensor_tensor(out=cols, in0=h[q][t][:, a:b], scalar=scalar, in1=cols, op0=MULT, op1=ADD)
 
-        z = [keep.tile([P, PACK * QUARTER], BF16, name=f"z{q}", align_bytes=64) for q in range(4)]
+        z = keep.tile([P, PACK * S], BF16, name="z", align_bytes=64)
 
-        def close_on_gpsimd(q):
-            cols = slice(QUARTER * q, QUARTER * (q + 1))
+        def close_on_gpsimd(a, b):
+            cols = slice(a, b)
             nc.gpsimd.tensor_tensor(
-                out=z[q][:].rearrange("p (c i t) -> p c t i", i=4, t=PACK),
+                out=z[:, PACK * a : PACK * b].rearrange("p (c i t) -> p c t i", i=4, t=PACK),
                 in0=sums[:, :, cols].rearrange("p t (c i) -> p c t i", i=4),
                 in1=near[:, :, cols].rearrange("p t (c i) -> p c t i", i=4),
                 op=ADD,
             )
 
-        def close_on_scalar(q, a, b):
+        def close_on_scalar(a, b):
             nc.scalar.activation(
-                out=z[q][:, PACK * a : PACK * b].rearrange("p (c i t) -> p c t i", i=4, t=PACK),
-                in_=sums[:, :, QUARTER * q + a : QUARTER * q + b].rearrange("p t (c i) -> p c t i", i=4),
+                out=z[:, PACK * a : PACK * b].rearrange("p (c i t) -> p c t i", i=4, t=PACK),
+                in_=sums[:, :, a:b].rearrange("p t (c i) -> p c t i", i=4),
                 func=COPY,
             )
 
@@ -242,7 +243,7 @@ def tile_picked_dconv_none_e_kernel(tc, xT, w1, w2_words, w2_scales, taps, offs,
         def second_product(q):
             z_codes = all_codes[:, QUARTER * q : QUARTER * (q + 1)]
             z_scales = keep.tile([P, QUARTER], U8, name=f"z_scales{q}", align_bytes=64)
-            nc.vector.quantize_mx(out=z_codes.bitcast(FP8X4), scales=z_scales[:], in_=z[q][:])
+            nc.vector.quantize_mx(out=z_codes.bitcast(FP8X4), scales=z_scales[:], in_=z[:, PACK * QUARTER * q : PACK * QUARTER * (q + 1)])
             acc = psum.tile([P, QUARTER], F32, name=f"acc{q}", tag=f"bank{2 + q}")
             nc.tensor.matmul_mx(
                 out=acc[:],
@@ -266,18 +267,20 @@ def tile_picked_dconv_none_e_kernel(tc, xT, w1, w2_words, w2_scales, taps, offs,
             add_tap(0, t, 1)
         for t in range(1, PACK):
             near_term(t < PACK - 1, 0, t)
-        close_on_gpsimd(0)
+        close_on_gpsimd(0, QUARTER)
         open_quarter(3)
         back_products(3, range(PACK))
         for t in range(PACK):
-            far_term(t >= 2, 1, t)
-        for t in range(PACK):
+            far_term(t < 2, 1, t)
+        for t in (2, 3, 0, 1):
             add_tap(1, t, 1)
         for t in (0, 1):
             far_term(True, 2, t)
-        for t in range(PACK):
+        for t in (2, 3, 0, 1):
             near_term(True, 1, t)
-        close_on_gpsimd(1)
+        close_on_gpsimd(QUARTER, QUARTER + SECOND)
+        for t in (2, 3, 0, 1):
+            add_near(1, t, SECOND, QUARTER, tap(t, 0))
         for t in (2, 3):
             far_term(True, 2, t)
         for d in (1, 0):
@@ -285,12 +288,12 @@ def tile_picked_dconv_none_e_kernel(tc, xT, w1, w2_words, w2_scales, taps, offs,
                 add_tap(2, t, d)
         for t in range(PACK):
             far_term(True, 3, t)
-        close_on_scalar(2, 0, QUARTER)
+        close_on_scalar(QUARTER + SECOND, 3 * QUARTER)
         for t in range(PACK):
             add_tap(3, t, 1)
         for a, b in ((0, QUARTER - LAST), (QUARTER - LAST, QUARTER)):
             for t in range(PACK):
-                add_near(t, a, b, last_tap[:] if a and t == 0 else tap(t, 0))
-            close_on_scalar(3, a, b)
+                add_near(3, t, a, b, last_tap[:] if a and t == 0 else tap(t, 0))
+            close_on_scalar(3 * QUARTER + a, 3 * QUARTER + b)
         for q in range(4):
             second_product(q)

@@ -28,7 +28,6 @@ HALF = S // 2
 QUARTER = S // 4
 NEAR_BYTES = 4 * PACK * HALF
 LAST = 64
-SECOND = 88
 
 
 def tile_picked_dconv_none_e_kernel(tc, xT, w1, w2_words, w2_scales, taps, offs, out):
@@ -207,8 +206,7 @@ def tile_picked_dconv_none_e_kernel(tc, xT, w1, w2_words, w2_scales, taps, offs,
             term(on_scalar, sums[:, t, cols], src, t, 2)
 
         def near_term(on_scalar, q, t):
-            count = SECOND if q else QUARTER
-            term(on_scalar, near[:, t, QUARTER * q : QUARTER * q + count], h[q][t][:, 0:count], t, 0)
+            term(on_scalar, near[:, t, QUARTER * q : QUARTER * (q + 1)], h[q][t], t, 0)
 
         nc.scalar.copy(out=last_tap[:], in_=tap(0, 0))
 
@@ -261,26 +259,23 @@ def tile_picked_dconv_none_e_kernel(tc, xT, w1, w2_words, w2_scales, taps, offs,
 
         far_term(False, 0, 0)
         near_term(False, 0, 0)
-        for t in range(PACK):
-            if t:
-                far_term(True, 0, t)
-            add_tap(0, t, 1)
+        add_tap(0, 0, 1)
         for t in range(1, PACK):
-            near_term(t < PACK - 1, 0, t)
+            far_term(True, 0, t)
+            add_tap(0, t, 1)
+            near_term(False, 0, t)
         close_on_gpsimd(0, QUARTER)
         open_quarter(3)
         back_products(3, range(PACK))
         for t in range(PACK):
-            far_term(t < 2, 1, t)
-        for t in (2, 3, 0, 1):
+            far_term(True, 1, t)
+        for t in range(PACK):
             add_tap(1, t, 1)
         for t in (0, 1):
             far_term(True, 2, t)
-        for t in (2, 3, 0, 1):
+        for t in range(PACK):
             near_term(True, 1, t)
-        close_on_gpsimd(QUARTER, QUARTER + SECOND)
-        for t in (2, 3, 0, 1):
-            add_near(1, t, SECOND, QUARTER, tap(t, 0))
+        close_on_gpsimd(QUARTER, HALF)
         for t in (2, 3):
             far_term(True, 2, t)
         for d in (1, 0):
@@ -288,7 +283,7 @@ def tile_picked_dconv_none_e_kernel(tc, xT, w1, w2_words, w2_scales, taps, offs,
                 add_tap(2, t, d)
         for t in range(PACK):
             far_term(True, 3, t)
-        close_on_scalar(QUARTER + SECOND, 3 * QUARTER)
+        close_on_scalar(HALF, 3 * QUARTER)
         for t in range(PACK):
             add_tap(3, t, 1)
         for a, b in ((0, QUARTER - LAST), (QUARTER - LAST, QUARTER)):

from contextlib import ExitStack

import concourse.mybir as mybir

K, T, S, D, H, N = 1024, 1024, 512, 3, 512, 128
FLOPS = 2 * K * H * S + 2 * H * N * S

F32 = mybir.dt.float32
BF16 = mybir.dt.bfloat16
I32 = mybir.dt.int32
U32 = mybir.dt.uint32
U16 = mybir.dt.uint16
U8 = mybir.dt.uint8
FP8X4 = mybir.dt.float8_e4m3fn_x4
COPY = mybir.ActivationFunctionType.Copy
MULT = mybir.AluOpType.mult
ADD = mybir.AluOpType.add

P = 128
PACK = 4
K_PASS = P * PACK
PASSES = K // K_PASS

X_PIECES = [(0, 0, 512, 256), (0, 512, 256, 128), (0, 768, 256, 128), (1, 0, 512, 256), (1, 512, 256, 128), (1, 768, 128, 128), (1, 896, 128, 0)]
W_PIECES = [(0, 0, 64, 64), (0, 64, 64, 64), (1, 0, 64, 64), (1, 64, 32, 0), (1, 96, 32, 12)]
W_ON_GPSIMD = (24,)
HALF = S // 2
QUARTER = S // 4
NEAR_BYTES = 4 * PACK * HALF
LAST = 64


def tile_picked_dconv_none_e_kernel(tc, xT, w1, w2_words, w2_scales, taps, offs, out):
    nc = tc.nc

    def cast(engine_is_scalar, dst, src):
        if engine_is_scalar:
            nc.scalar.activation(out=dst, in_=src, func=COPY)
        else:
            nc.vector.tensor_copy(out=dst, in_=src)

    with ExitStack() as ctx:
        keep = ctx.enter_context(tc.tile_pool(name="keep", bufs=1))
        reuse = ctx.enter_context(tc.tile_pool(name="reuse", bufs=1))
        psum = ctx.enter_context(tc.psum_pool(name="psum", bufs=1))

        offsets = keep.tile([P, S // 16], U16, name="offsets")
        taps_sb = keep.tile([P, PACK * D], F32, name="taps_sb")
        x_raw = []
        for n, (g, t0, nt, ns) in enumerate(X_PIECES):
            raw = keep.tile([P, PACK, nt], F32, name=f"x_raw{n}")
            rows = xT[g * K_PASS : (g + 1) * K_PASS, t0 : t0 + nt]
            nc.sync.dma_start(out=raw[:], in_=rows.rearrange("(p j) c -> p j c", j=PACK))
            x_raw.append(raw)
            if n == 0:
                nc.sync.dma_start(offsets[:], offs)
        w_raw = []
        for n, (g, m0, nm, ns) in enumerate(W_PIECES):
            raw = keep.tile([P, PACK, PACK * nm], F32, name=f"w_raw{n}")
            rows = w1[g * K_PASS : (g + 1) * K_PASS, PACK * m0 : PACK * (m0 + nm)]
            nc.sync.dma_start(out=raw[:], in_=rows.rearrange("(p j) c -> p j c", j=PACK))
            w_raw.append(raw)

        x_scales = keep.tile([P, T], U8, name="x_scales", align_bytes=64)
        nc.vector.memset(x_scales[:].bitcast(I32), 0)
        nc.sync.dma_start(out=taps_sb[:], in_=taps.rearrange("(p t) d -> p (t d)", t=PACK))
        w2_plane = keep.tile([P, N], U8, name="w2_plane", align_bytes=64)
        nc.vector.memset(w2_plane[:].bitcast(I32), 0)
        w2_codes = keep.tile([P, N], U32, name="w2_codes", align_bytes=64)
        nc.sync.dma_start(out=w2_codes[:].bitcast(I32), in_=w2_words[0].rearrange("p n t -> p (n t)").bitcast(I32))
        for q in range(4):
            nc.sync.dma_start(
                out=w2_plane[32 * q : 32 * q + 4, :].bitcast(I32),
                in_=w2_scales[0, 4 * q : 4 * q + 4, :].bitcast(I32),
            )

        sums = keep.tile([P, PACK, S], F32, name="sums")
        near = reuse.tile([P, PACK, HALF], F32, name="near", offset=0, align_bytes=64)
        last_tap = reuse.tile([P, 1], F32, name="last_tap", offset=NEAR_BYTES, align_bytes=64)
        nc.vector.memset(sums[:, :, 0:2], 0.0)

        x_codes = [keep.tile([P, T], U32, name=f"x_codes{g}", align_bytes=64) for g in range(PASSES)]
        picked_codes = [keep.tile([P, S], U32, name=f"picked_codes{g}", align_bytes=64) for g in range(PASSES)]
        picked_scales = keep.tile([P, S], U8, name="picked_scales", align_bytes=64)

        def pick_scales():
            nc.vector.tensor_copy(out=picked_scales[:], in_=x_scales[:].indirect(offsets[:]))

        for n, (g, t0, nt, ns) in enumerate(X_PIECES):
            shares = [share for share in ((False, ns, nt), (True, 0, ns)) if share[2] > share[1]]
            grouped = [keep.tile([P, PACK * (b - a)], BF16, name=f"x_grouped{n}_{a}", align_bytes=64) for on_scalar, a, b in shares]
            for (on_scalar, a, b), dst in zip(shares, grouped):
                cast(
                    on_scalar,
                    dst[:].rearrange("p (c i j) -> p c j i", i=4, j=PACK),
                    x_raw[n][:, :, a:b].rearrange("p j (c i) -> p c j i", i=4),
                )
            for (on_scalar, a, b), src in zip(shares, grouped):
                nc.vector.quantize_mx(
                    out=x_codes[g][:, t0 + a : t0 + b].bitcast(FP8X4),
                    scales=x_scales[PACK * g : P, t0 + a : t0 + b],
                    in_=src[:],
                )
            if t0 + nt == T:
                if g == PASSES - 1:
                    pick_scales()
                nc.vector.tensor_copy(out=picked_codes[g][:], in_=x_codes[g][:].indirect(offsets[:]))

        w_codes = [keep.tile([P, H], U32, name=f"w_codes{g}", align_bytes=64) for g in range(PASSES)]
        w_scales = [keep.tile([P, H], U8, name=f"w_scales{g}", align_bytes=64) for g in range(PASSES)]

        def cast_w(n, grouped, base):
            g, m0, nm, ns = W_PIECES[n]
            shares = [("scalar", ns), ("vector", nm - ns)]
            if n == 1:
                shares = [("gpsimd", count) for count in W_ON_GPSIMD] + [("scalar", nm - sum(W_ON_GPSIMD))]
            a = 0
            for engine, count in shares:
                b = a + count
                if count:
                    dst = grouped[:, :, PACK * (m0 - base + a) : PACK * (m0 - base + b)].rearrange("p t (m j) -> p m j t", j=PACK)
                    src = w_raw[n][:, :, PACK * a : PACK * b].rearrange("p j (m t) -> p m j t", t=PACK)
                    if engine == "gpsimd":
                        nc.gpsimd.tensor_scalar(out=dst.rearrange("p m j t -> p t m j"), in0=src.rearrange("p m j t -> p t m j"), scalar1=1.0, scalar2=0.0, op0=MULT, op1=ADD)
                    elif engine == "vector":
                        cast(False, dst.rearrange("p m j t -> p m t j"), src.rearrange("p m j t -> p m t j"))
                    else:
                        cast(True, dst, src)
                a = b

        def quantize_w(g, grouped, base, nm, t, count=1):
            cols = slice(P * t + base, P * (t + count - 1) + base + nm)
            nc.vector.quantize_mx(
                out=w_codes[g][:, cols].bitcast(FP8X4),
                scales=w_scales[g][:, cols],
                in_=grouped[:, t : t + count, :].rearrange("p t c -> p (t c)"),
            )

        h = [[psum.tile([P, QUARTER], F32, name=f"h0_{t}", tag=f"bank{t}")[:] for t in range(PACK)]]

        def open_quarter(q):
            banks = [psum.tile([P, 2, QUARTER], F32, name=f"h{q}_pair{u}", tag=f"bank{(2 * q + 2 + u) % 8}") for u in range(2)]
            h.append([banks[t // 2][:, t % 2, :] for t in range(PACK)])

        def first_product(g, q, t, start, stop):
            cols = slice(P * t, P * (t + 1))
            entries = slice(QUARTER * q, QUARTER * (q + 1))
            nc.tensor.matmul_mx(
                out=h[q][t],
                lhsT=w_codes[g][:, cols].bitcast(FP8X4),
                lhsT_scale=w_scales[g][:, cols],
                rhs=picked_codes[g][:, entries].bitcast(FP8X4),
                rhs_scale=picked_scales[PACK * g : P, entries],
                start=start,
                stop=stop,
            )

        open_quarter(1)
        open_quarter(2)
        first = keep.tile([P, PACK, P * PACK], BF16, name="w_first", tag="w_shared", align_bytes=64)
        for n, piece in enumerate(W_PIECES):
            if piece[0] == 0:
                cast_w(n, first, 0)
        for t0, count in ((0, 1), (1, 1), (2, 2)):
            quantize_w(0, first, 0, P, t0, count)
            for t in range(t0, t0 + count):
                first_product(0, 0, t, True, False)
                first_product(0, 1, t, t % 2 == 0, False)
        low = keep.tile([P, PACK, 64 * PACK], BF16, name="w_low", align_bytes=64)
        high = keep.tile([P, PACK, 64 * PACK], BF16, name="w_high", tag="w_high", align_bytes=64)
        for n, piece in enumerate(W_PIECES):
            if piece[0] == 1 and piece[1] < 64:
                cast_w(n, low, 0)
        for n, piece in enumerate(W_PIECES):
            if piece[0] == 1 and piece[1] >= 64:
                cast_w(n, high, 64)
        for t in range(PACK):
            quantize_w(1, low, 0, 64, t)
            quantize_w(1, high, 64, 64, t)
            first_product(1, 0, t, False, True)
        for t in range(PACK):
            first_product(1, 1, t, False, t % 2 == 1)

        def back_products(q, tiles):
            for t in tiles:
                first_product(1, q, t, True, False)
                first_product(0, q, t, False, True)

        back_products(2, range(PACK))

        def tap(t, d):
            return taps_sb[:, D * t + d : D * t + d + 1]

        def term(on_scalar, dst, src, t, d):
            if on_scalar:
                nc.scalar.activation(out=dst, in_=src, func=COPY, scale=tap(t, d))
            else:
                nc.vector.tensor_scalar(out=dst, in0=src, scalar1=tap(t, d), scalar2=None, op0=MULT)

        def h_cols(q, t, d):
            count = min(QUARTER, S - d - QUARTER * q)
            return h[q][t][:, 0:count], slice(QUARTER * q + d, QUARTER * q + d + count)

        def far_term(on_scalar, q, t):
            src, cols = h_cols(q, t, 2)
            term(on_scalar, sums[:, t, cols], src, t, 2)

        def near_term(on_scalar, q, t):
            term(on_scalar, near[:, t, QUARTER * q : QUARTER * (q + 1)], h[q][t], t, 0)

        nc.scalar.copy(out=last_tap[:], in_=tap(0, 0))

        def add_tap(q, t, d):
            src, cols = h_cols(q, t, d)
            nc.vector.scalar_tensor_tensor(out=sums[:, t, cols], in0=src, scalar=tap(t, d), in1=sums[:, t, cols], op0=MULT, op1=ADD)

        def add_near(q, t, a, b, scalar):
            cols = sums[:, t, QUARTER * q + a : QUARTER * q + b]
            nc.vector.scalar_tensor_tensor(out=cols, in0=h[q][t][:, a:b], scalar=scalar, in1=cols, op0=MULT, op1=ADD)

        z = keep.tile([P, PACK * S], BF16, name="z", align_bytes=64)

        def close_on_gpsimd(a, b):
            cols = slice(a, b)
            nc.gpsimd.tensor_tensor(
                out=z[:, PACK * a : PACK * b].rearrange("p (c i t) -> p c t i", i=4, t=PACK),
                in0=sums[:, :, cols].rearrange("p t (c i) -> p c t i", i=4),
                in1=near[:, :, cols].rearrange("p t (c i) -> p c t i", i=4),
                op=ADD,
            )

        def close_on_scalar(a, b):
            nc.scalar.activation(
                out=z[:, PACK * a : PACK * b].rearrange("p (c i t) -> p c t i", i=4, t=PACK),
                in_=sums[:, :, a:b].rearrange("p t (c i) -> p c t i", i=4),
                func=COPY,
            )

        all_codes = reuse.tile([P, S], U32, name="z_codes", offset=NEAR_BYTES + 64 - 4 * S, align_bytes=64)

        def second_product(q):
            z_codes = all_codes[:, QUARTER * q : QUARTER * (q + 1)]
            z_scales = keep.tile([P, QUARTER], U8, name=f"z_scales{q}", align_bytes=64)
            nc.vector.quantize_mx(out=z_codes.bitcast(FP8X4), scales=z_scales[:], in_=z[:, PACK * QUARTER * q : PACK * QUARTER * (q + 1)])
            acc = psum.tile([P, QUARTER], F32, name=f"acc{q}", tag=f"bank{2 + q}")
            nc.tensor.matmul_mx(
                out=acc[:],
                lhsT=w2_codes[:].bitcast(FP8X4),
                lhsT_scale=w2_plane[:],
                rhs=z_codes.bitcast(FP8X4),
                rhs_scale=z_scales[:],
                start=True,
                stop=True,
            )
            result = keep.tile([P, QUARTER], F32, name=f"result{q}")
            nc.scalar.activation(out=result[:], in_=acc[:], func=COPY)
            queue = nc.scalar if q == 3 else nc.sync
            queue.dma_start(out=out[:, QUARTER * q : QUARTER * (q + 1)], in_=result[:])

        far_term(False, 0, 0)
        near_term(False, 0, 0)
        add_tap(0, 0, 1)
        for t in range(1, PACK):
            far_term(True, 0, t)
            add_tap(0, t, 1)
            near_term(False, 0, t)
        close_on_gpsimd(0, QUARTER)
        open_quarter(3)
        back_products(3, range(PACK))
        for t in range(PACK):
            far_term(True, 1, t)
        for t in range(PACK):
            add_tap(1, t, 1)
        for t in (0, 1):
            far_term(True, 2, t)
        for t in range(PACK):
            near_term(True, 1, t)
        close_on_gpsimd(QUARTER, HALF)
        for t in (2, 3):
            far_term(True, 2, t)
        for d in (1, 0):
            for t in range(PACK):
                add_tap(2, t, d)
        for t in range(PACK):
            far_term(True, 3, t)
        close_on_scalar(HALF, 3 * QUARTER)
        for t in range(PACK):
            add_tap(3, t, 1)
        for a, b in ((0, QUARTER - LAST), (QUARTER - LAST, QUARTER)):
            for t in range(PACK):
                add_near(3, t, a, b, last_tap[:] if a and t == 0 else tap(t, 0))
            close_on_scalar(3 * QUARTER + a, 3 * QUARTER + b)
        for q in range(4):
            second_product(q)
